import numpy as np, ml_dtypes
CORES = [51,54,179,182]
N = 4
BF = ml_dtypes.bfloat16
V, G, RO, RW, TU, TD = 1536, 192, 6, 1, 3, 2
W = V + (N - 1) * G
def parts(rng):
    S = rng.integers(0, W, (N, 8, 16, V)); T = rng.integers(0, W, (N, 8, 16, V))
    cs = rng.integers(0, 16, (N, 8, V)); ct = rng.integers(0, 16, (N, 8, V))
    return S, T, cs, ct, rng.integers(-256, 257, (N, 8, 16, V)) * 0.00390625
def pack(S, T, cs, ct, s):
    return {"s0": np.ascontiguousarray(s.reshape(N, 128, V)).astype(BF), "pt": (S + 4096 * T).reshape(N, 128, V).astype(np.int32), "cur": (cs + 16 * ct).astype(np.int32)}
def plant(S, T, cs, ct, s):
    def put(v, a, b):
        np.put_along_axis(S[..., v], cs[..., v][..., None], a, 2); np.put_along_axis(T[..., v], ct[..., v][..., None], b, 2)
    s[..., 1] = 0.25; put(1, W - 1, 0); s[..., 3] = 1.0; put(3, 3, 3)
    for k in range(17):
        m = 16 + k; s[:, ::2, :k, m] = -1.0; s[:, 1::2, :k, m] = -2.0 ** -20; s[:, :, k:, m] = 0.5; put(m, 1, m)
        for v in (40 + 2 * k, V - 33 + 2 * k): s[..., v] = -1.0; put(v, 1, m)
        for v in (41 + 2 * k, V - 34 + 2 * k): s[..., v] = 1.0; put(v, 3, m)
    for j in range(8):
        for e in (80 + 3 * j, V - 64 + 3 * j):
            s[..., e] = 0.130859375; s[..., e + 1] = 0.9140625; s[..., e + 2] = 0.1875
            put(e, 1, e + 2); put(e + 1, e, e + 1); put(e + 2, e + 1, e + 2)
    for h in (106, V - 72):
        o, g, b, e, a, v, x = range(h, h + 7)
        for m, t in ((o, 0.0), (g, 0.96484375), (b, 0.388671875), (e, 0.58984375), (a, 0.84765625), (v, 0.000732421875), (x, -1.0)): s[..., m] = t
        put(o, o, o); put(g, o, g); put(b, g, b); put(e, o, e); put(a, e, a); put(v, a, 32); put(x, x, v)
        np.put_along_axis(S[..., v], ((cs[..., v] + 1) & 15)[..., None], b, 2)
def setup_inputs(rng):
    return pack(*parts(rng))
def setup_inputs_spread(rng):
    S, T, cs, ct, s = parts(rng)
    s = s * np.exp2(rng.integers(-2, 1, (N, 8, 1, V))) * (rng.random((N, 8, 1, V)) > 0.0625)
    S = np.minimum((W * rng.random(S.shape) ** 2).astype(np.int64), W - 1); T = W - 1 - np.minimum((W * rng.random(T.shape) ** 3).astype(np.int64), W - 1)
    cs = np.minimum((16 * rng.random(cs.shape) ** 3).astype(np.int64), 15); ct = 15 - np.minimum((16 * rng.random(ct.shape) ** 3).astype(np.int64), 15)
    return pack(S, T, cs, ct, s)
def setup_inputs_ends(rng):
    S, T, cs, ct, s = parts(rng)
    u = rng.random(S.shape); lo, hi = 0, W - 1
    S = np.where(u < 0.36, lo, np.where(u < 0.72, hi, np.where(u < 0.79, lo, np.where(u < 0.86, hi, S))))
    T = np.where(u < 0.36, lo, np.where(u < 0.72, hi, np.where(u < 0.79, hi, np.where(u < 0.86, lo, T))))
    u = rng.random(cs.shape)
    cs = np.where(u < 0.36, 0, np.where(u < 0.72, 15, np.where(u < 0.79, 0, np.where(u < 0.86, 15, cs))))
    ct = np.where(u < 0.36, 0, np.where(u < 0.72, 15, np.where(u < 0.79, 15, np.where(u < 0.86, 0, ct))))
    sg = np.where(rng.random((N, 8, 1, V)) < 0.5, rng.integers(0, 2, (N, 8, 1, V)), rng.integers(0, 2, s.shape)) * 2.0 - 1.0
    m = rng.random((N, 8, 1, V)) < 0.7; m[..., 0] = False; m[..., G - 1] = False
    s = np.where(m, sg, s); plant(S, T, cs, ct, s)
    return pack(S, T, cs, ct, s)
def setup_inputs_corners(rng):
    S, T, cs, ct, s = parts(rng); v = np.arange(V); z = 0 * v
    tbl = np.stack([v, (v - 1) % V, (v + 1) % V, V - 1 - v, z, z + V - 1, z + V, z + W - 1, z + G - 1, V + v % G, W - 1 - v % G, v % G])
    S = np.where(rng.random(S.shape) < 0.25, S, tbl[rng.integers(0, len(tbl), (N, 8, 16))])
    T = np.where(rng.random(T.shape) < 0.25, T, tbl[rng.integers(0, len(tbl), (N, 8, 16))])
    e = np.array([0, 1, 14, 15]); cs = rng.choice(e, cs.shape); ct = rng.choice(e, ct.shape)
    s = np.where(rng.random(s.shape) < 0.7, rng.choice(np.array([0.0, 0.25, -0.25, 0.5, -0.5, 1.0, -1.0]), s.shape), s)
    plant(S, T, cs, ct, s)
    return pack(S, T, cs, ct, s)
def setup_inputs_crowd(rng):
    S, T, cs, ct, s = parts(rng); pl = np.array([0, G - 1, G, V - 1, V, W - 1]); g = np.arange(8).reshape(1, 8, 1, 1); v = np.arange(V); home = (g == 4) | (g == 7)
    for X in (S, T):
        same = np.where(home, rng.choice(pl[:4], (N, 8, 16, 1)), rng.choice(pl, (N, 8, 16, 1)))
        few = np.where(home, rng.choice(pl[:4], X.shape), rng.choice(pl, X.shape)); but = rng.integers(0, V, (N, 8, 16, 1))
        X[...] = np.where(g % 4 == 3, few, np.where((g % 2 == 1) & (v == but), X, same))
    s[:, 4] = s[:, 4, :1] + 0.0; s[:, 7, :15] = s[:, 7, :1] + 0.0
    return pack(S, T, cs, ct, s)
def setup_inputs_calm(rng):
    S, T, cs, ct, s = parts(rng); r = np.arange(N).reshape(N, 1, 1); g = np.arange(8).reshape(1, 8, 1)
    cs = 0 * cs + (g + r) % 4; ct = 0 * ct + (g // 2 + r) % 4
    share = np.array([0.97, 0.95, 0.9, 0.8]).reshape(1, 4, 1, 1); share = np.concatenate([share, share], axis=1)
    return pack(S, T, cs, ct, np.where(rng.random(s.shape) < share, 0.5, s))
def check_ranges(d):
    bad = []; p = np.asarray(d["pt"]).astype(np.int64); c = np.asarray(d["cur"]).astype(np.int64); a = np.abs(np.asarray(d["s0"]).astype(np.float64))
    if np.min(p) < 0 or np.max(p) > 4097 * (W - 1) or np.max(p & 4095) > W - 1 or np.max(p >> 12) > W - 1: bad.append("range of pt")
    if np.min(c) < 0 or np.max(c) > 255: bad.append("range of cur")
    if not np.all((a == 0) | ((a >= 2.0 ** -20) & (a <= 1))): bad.append("size of s0")
    return bad
def pick(t, ix):
    out = []
    for r in range(N):
        w = [t[r]] + [t[(r - d) % N][(np.arange(8) + d * (d + 1) // 2) % 8][..., :G] for d in range(1, N)]
        out.append(np.take_along_axis(np.concatenate(w, axis=2), ix[r][:, None, :], 2))
    return np.stack(out)
def reference(s0, pt, cur):
    s = s0.astype(np.float32).reshape(N, 8, 16, V); y = s.astype(np.float64); c = np.zeros(s.shape, np.int64)
    p = pt.astype(np.int64).reshape(N, 8, 16, V); S = p & 4095; T = p >> 12
    cs = cur.astype(np.int64) & 15; ct = cur.astype(np.int64) >> 4; row = np.arange(16).reshape(1, 1, 16, 1)
    for step in range(RO):
        a = np.take_along_axis(S, cs[:, :, None], 2)[:, :, 0]; b = np.take_along_axis(T, ct[:, :, None], 2)[:, :, 0]
        sa, ya, cb = pick(s, a), pick(y, a), pick(c, b)
        new = np.float32(1) - np.float32(2) * np.abs(sa * s)
        z = np.add.reduce(np.where(s >= 0, cb, -cb), axis=2)
        hold = z <= -TD
        y = np.where(hold[:, :, None], y, np.tanh((1.0 + ya) * new))
        if step < RO - 1:
            via = np.take_along_axis(a, np.minimum(a, V - 1), 2)
            m = (a < V) & (z >= RW) & (z < TU)
            S = np.where(m[:, :, None] & (row == cs[:, :, None]), via[:, :, None], S)
        c = ((s < 0) & (new >= 0)).astype(np.int64) - ((s >= 0) & (new < 0)).astype(np.int64)
        cs = (cs + (z >= TU)) & 15; ct = (ct + hold) & 15; s = new
    return {"y": y.reshape(N, 128, V).astype(np.float32), "q": (cs + 16 * ct).astype(np.float32)}

def check_inputs(d):
    bad = list(check_ranges(d))
    if not bad:
        for name, y in reference(**d).items():
            for q in range(N):
                v = np.abs(np.asarray(y[q], np.float64)); s = np.sqrt(np.mean(v * v))
                if v.max() > 4 * s or s < 2.0 ** -2: bad.append('%s of rank %d is uneven or too small' % (name, q))
    return bad

@@ -1,0 +1,641 @@
+import numpy as np
+from concourse.bass import DstId, RemoteDMATransfer
+from concourse.mybir import AluOpType as OP, ActivationFunctionType as AF
+
+V, NB, W, C, K = 1536, 192, 2112, 512, 96
+SH = {1: 1, 2: 3, 3: 6}
+CH = [(0, 192), (192, 864), (864, 1536)]
+SV = {}
+EPS = 2.0 ** -26
+CYC, PEC, GA, DMA, FAR, HOP, SOON = 0.0009, 0.6, 1.56, 2.0, 4.5, 0.12, 0.25
+FIX = {"v": 0.04, "a": 0.1, "p": 0.1, "g": 0.15}
+SELF, TRIES = 0.08, 6000
+CASES = [(1.56, 1.0, 1.0), (1.15, 1.2, 0.7), (2.0, 0.75, 1.4)]
+WD = [b - a for a, b in CH]
+ORDER = []
+F, B, H, I, U = "float32", "bfloat16", "float16", "int32", "uint16"
+
+
+def sb(n, d):
+    return ("sbuf", [128, n], d)
+
+
+SCRATCH = {
+    "ptb": sb(V, I), "si": sb(2 * C, I), "sf": sb(V, H), "oh0": sb(V, B), "oh1": sb(V, B),
+    "ra": sb(V, H), "rb0": sb(V, H), "rb1": sb(V, H),
+    "pp": sb(V, F), "xx": sb(V, F), "zp": sb(V, B), "aq": sb(9 * V, B), "mv": sb(V, F),
+    "sp0": sb(V, F), "sp1": sb(V, F),
+    "t4": sb(384, I), "e4": sb(384, F), "one": sb(128, F), "bd1": sb(128, F), "bd": sb(128, F), "c1": sb(K, F), "rr": sb(K, I),
+    "ci": sb(144, F), "gi": sb(128, F), "lw": sb(128, F), "pc": sb(4, I), "col": sb(16, F),
+    "zb": sb(3 * 144, B), "zh": sb(5 * 144, H), "mb": sb(6 * 128, B), "mh": sb(128, H),
+    "curb": sb(K, I), "ci2": sb(2 * K, I), "ft": sb(4 * K, B),
+    "vs": sb(4 * K, F), "qs": sb(5 * K, F), "qt": sb(5 * K, F),
+    "qh": sb(5 * K, B), "ql": sb(5 * K, B), "c0": sb(2 * K, F), "ti": sb(2 * K, I), "tj": sb(2 * K, I),
+    "tf": sb(2 * K, F), "pa": sb(K, F), "thr": sb(K, F), "dd": sb(2 * K, F), "pr": sb(2 * K, F),
+    "l2": sb(K, F), "nx": sb(K, F), "nx2": sb(K, F), "jj": sb(2 * K, F), "bs": sb(2 * K, F),
+    "be": sb(K, F), "bp": sb(K, F), "dt": sb(4 * K, F), "f2": sb(3 * K, F), "db": sb(K, F),
+    "ga": sb(2 * K, F), "qq": sb(2 * K, F), "qb": sb(K, B),
+    "la": sb(6 * K, U), "ll": sb(K, U), "lb": sb(12 * K, U),
+    "df": ("dram", [6, 256, NB], F), "dh": ("dram", [7, 256, NB], B),
+}
+for _j in range(3):
+    SCRATCH["m%d" % _j] = sb(W, F)
+    SCRATCH["yy%d" % _j] = sb(W, F)
+    SCRATCH["cc%d" % _j] = sb(W, B)
+    SCRATCH["hh%d" % _j] = sb(V, B)
+    SCRATCH["ver%d" % _j] = sb(6 * (CH[_j][1] - CH[_j][0]), F)
+for _j in range(8):
+    SCRATCH["b%d" % _j] = ("psum", [128, C], F)
+
+SEMAPHORES = (["ev", "ea", "ep", "eg", "out", "as1"] + ["hin%d" % t for t in range(2, 7)]
+              + ["a%s%d" % (k, t) for k in "mcy" for t in range(2, 7)] + ["d%d" % j for j in range(95)])
+
+
+def helpers(core, T, topo):
+    return [c for c in topo.cores_of(core) if topo.die(c) == topo.die(core) and T.rank_of(c) is None][:3]
+
+
+def mask_of(engines):
+    return sum(1 << e for e in engines)
+
+
+def spread(g, core, T, topo, rank, stage, window, sem, local):
+    n = len(T.cores)
+    dst = {d: T.cores[(rank + d) % n] for d in SH}
+    narrow = min((topo.engines(core, dst[d]) for d in SH), key=len)
+    far = [d for d in SH if len(topo.engines(core, dst[d])) == len(narrow)]
+    trs, sent = [], 0
+    for d in SH:
+        if d in far:
+            q = far.index(d)
+            eng = narrow[q * len(narrow) // len(far):(q + 1) * len(narrow) // len(far)]
+        else:
+            eng = [e for e in topo.engines(core, dst[d]) if e not in narrow]
+        rid, pid = topo.addr(dst[d], core)
+        trs.append(RemoteDMATransfer(dst_ids=[DstId(rid=rid, pnc=pid)], dma_engine_mask=mask_of(eng), remote_sem=sem,
+                                     src=stage[16 * SH[d]:16 * SH[d] + 128, :], dst=window[:, V + (d - 1) * NB:V + d * NB]))
+        sent += len(eng)
+    g.remote_dma_fused(trs, local_sem=local)
+    return sent
+
+
+def arrange(ops):
+    n = len(ops)
+    qs = [o["q"] for o in ops]
+    deps = [list(o["deps"].items()) for o in ops]
+    kids = [[] for _ in ops]
+    for i in range(n):
+        for j, hard in deps[i]:
+            kids[j].append((i, hard))
+
+    def costs(ga, dm, pc):
+        busy, lat = [], []
+        for o in ops:
+            f = ga / GA if o["gather"] else pc if o["q"] == "p" else 1.0
+            busy.append(o["busy"] * f)
+            lat.append(o["lat"] * (dm if o["sem"] else f))
+        return busy, lat
+
+    cases = [costs(*c) for c in CASES]
+
+    move = [o["move"] for o in ops]
+    firm = [[(j, HOP if qs[j] != qs[i] else SELF) for j, hard in deps[i] if hard] for i in range(n)]
+
+    def ends(seq):
+        out = 0.0
+        for busy, lat in cases:
+            free, done, pipe = dict.fromkeys("vapgsx", 0.0), [0.0] * n, 0.0
+            for i in seq:
+                t = free[qs[i]]
+                for j, gap in firm[i]:
+                    if done[j] + gap > t:
+                        t = done[j] + gap
+                free[qs[i]] = t + busy[i]
+                done[i] = t + lat[i]
+                if move[i]:
+                    pipe = max(pipe + move[i], done[i])
+                    done[i] = pipe
+            out += max(done)
+        return out / len(cases)
+
+    def build(bonus, case):
+        busy, lat = case
+        rest = list(lat)
+        for i in range(n - 1, -1, -1):
+            rest[i] += bonus[i]
+            for j, hard in deps[i]:
+                rest[j] = max(rest[j], lat[j] + HOP + rest[i])
+        need, ready, free = [len(d) for d in deps], [0.0] * n, dict.fromkeys("vapgsx", 0.0)
+        cand, seq, pipe = {q: [] for q in free}, [], 0.0
+        for i in range(n):
+            if not need[i]:
+                cand[qs[i]].append(i)
+        while len(seq) < n:
+            t0, q = min((max(free[q], min(ready[i] for i in c)), q) for q, c in cand.items() if c)
+            i = max((j for j in cand[q] if ready[j] <= t0 + SOON), key=lambda j: (rest[j] - 2 * max(0.0, ready[j] - t0), -j))
+            cand[q].remove(i)
+            seq.append(i)
+            t = max(t0, ready[i])
+            free[q] = t + busy[i]
+            done = t + lat[i]
+            if move[i]:
+                pipe = done = max(pipe + move[i], done)
+            for k, hard in kids[i]:
+                ready[k] = max(ready[k], done + (HOP if qs[k] != q else SELF) if hard else t + busy[i])
+                need[k] -= 1
+                if not need[k]:
+                    cand[qs[k]].append(k)
+        return seq
+
+    rng = np.random.RandomState(1)
+    bonus = [0.0] * n
+    best = build(bonus, cases[0])
+    score = ends(best)
+    for it in range(TRIES):
+        trial = list(bonus)
+        for i in rng.randint(0, n, 6):
+            trial[i] = max(0.0, trial[i] + float(rng.normal()) * 2.5)
+        seq = build(trial, cases[0])
+        s = ends(seq)
+        if s <= score:
+            bonus, best, score = trial, seq, s
+    return best
+
+
+def helper_program(g, core, T, topo, rank, j):
+    sent = 0
+    for t in range(2, 7):
+        g.wait_ge(T.sem["hin%d" % t], 2 * len(topo.engines(T.cores[rank], core)))
+        sent += spread(g, core, T, topo, rank, (T.dh if j == 1 else T.df)[t - 1], T["%s%d" % (("m", "cc", "yy")[j], t % 3)],
+                       T.sem["a%s%d" % ("mcy"[j], t)], T.sem.out)
+    g.wait_ge(T.sem.out, sent)
+
+
+def rank_program(g, core, T, topo):
+    rank = T.rank_of(core)
+    if rank is None:
+        for r, c in enumerate(T.cores):
+            hs = helpers(c, T, topo)
+            if core in hs:
+                helper_program(g, core, T, topo, r, hs.index(core))
+        return
+    hs = helpers(core, T, topo)
+    nall = max(len(topo.engines(core, c)) for c in T.cores if c != core)
+    Q = {"v": g.vector, "a": g.scalar, "p": g.tensor, "g": g, "s": g.sync}
+    ops, last, readers, nd = [], {}, {}, [0]
+
+    def add(q, fn, r, w, busy, lat, sem=None, move=0.0):
+        deps = {}
+        for k in list(w) + [k for k in r if k[0] == "#"]:
+            for j in readers.get(k, []) + ([last[k]] if k in last else []):
+                if k in w or ops[j]["q"] != q:
+                    deps[j] = ops[j]["q"] != q or ops[j]["sem"] is not None
+        for k in r:
+            if k in last:
+                deps[last[k]] = True
+        for k in w:
+            if k[0] == "~" and k in last:
+                deps[last[k]] = False
+        ops.append(dict(q=q, fn=fn, deps=deps, busy=busy, lat=lat, sem=sem, move=move,
+                        gather=sem is None and any(k[:2] in ("la", "lb", "ll") for k in r)))
+        for k in r:
+            readers.setdefault(k, []).append(len(ops) - 1)
+        for k in w:
+            last[k] = len(ops) - 1
+            readers[k] = []
+
+    def op(q, fn, r, w, n=K):
+        us = max(n, 64) * CYC + FIX[q]
+        add(q, lambda s: fn().then_inc(s, 1), r, w, us, us)
+
+    def fill(ap, x, w):
+        op("v", lambda: g.vector.memset(ap, x), [], w)
+
+    def newsem(n):
+        nd[0] += 1
+        return ("d%d" % (nd[0] - 1), n)
+
+    def dma(q, out, in_, r, w, us=0.15, **kw):
+        add(q, lambda s: Q[q].dma_start(out, in_, **kw).then_inc(s, 16), r, w, 1.0 if q == "g" else 0.06,
+            DMA + us + (1.0 if q == "g" else 0.0), newsem(16), us)
+
+    def send(j, srcs, stage, t, r):
+        rid, pid = topo.addr(hs[j], core)
+        e = topo.engines(core, hs[j])
+        tr = RemoteDMATransfer(dst_ids=[DstId(rid=rid, pnc=pid)] * 2, dma_engine_mask=mask_of(e),
+                               remote_sem=T.sem["hin%d" % (t + 1)], srcs=srcs, dsts=[stage[t, 0:128, :], stage[t, 128:256, :]],
+                               alu_op=1 if len(srcs) > 1 else 0)
+        add("g", lambda s: g.remote_dma_fused([tr], local_sem=s), r, ["sent%d.%d" % (j, t)], 0.4, DMA + 1.0, newsem(len(e)))
+
+    def arrives(key, s, j, t, us=FAR):
+        add("x", None, ["sent%d.%d" % (j, t)], [key], 0.0, us, (s, nall))
+
+    def ts(out, in0, s1, s2, o0, o1, r, w, n=K):
+        if o1 is None:
+            op("v", lambda: g.vector.tensor_scalar(out, in0, s1, None, o0), r, w, n)
+        else:
+            op("v", lambda: g.vector.tensor_scalar(out, in0, s1, s2, o0, o1), r, w, n)
+
+    def tt(out, a, b, o, r, w, n=K):
+        op("v", lambda: g.vector.tensor_tensor(out, a, b, o), r, w, n)
+
+    def cp(out, a, r, w, n=K):
+        op("v", lambda: g.vector.tensor_copy(out, a), r, w, n)
+
+    def act(out, a, f, r, w, bias=0.0, scale=1.0, n=K):
+        op("a", lambda: g.scalar.activation(out, a, f, bias=bias, scale=scale), r, w, n)
+
+    def pe(mms, r, w, n):
+        def run():
+            for a in mms:
+                ins = g.tensor.matmul(*a)
+            return ins
+        op("p", run, r, w, n * PEC)
+
+    def iota(out, pat, base, cm, w, flt=True):
+        if flt:
+            op("g", lambda: g.iota(out, pat, base, cm, allow_small_or_imprecise_dtypes=True), [], w, 256)
+        else:
+            op("g", lambda: g.iota(out, pat, base, cm), [], w, 256)
+
+    def sel(out, a, pat, base, cm, r, w):
+        op("g", lambda: g.affine_select(out, a, pat, OP.is_ge, 0.0, base, cm), r, w, 256)
+
+    def issue():
+        if not ORDER:
+            ORDER.extend(arrange(ops))
+        total, tok, waited = {}, {}, {q: {} for q in Q}
+        for i in ORDER:
+            o = ops[i]
+            q = o["q"]
+            s, c = o["sem"] or ("e" + q, total.get("e" + q, 0) + 1)
+            total[s] = c
+            tok[i] = (s, c)
+            if q == "x":
+                continue
+            want = {}
+            for j, hard in o["deps"].items():
+                if hard:
+                    want[tok[j][0]] = max(want.get(tok[j][0], 0), tok[j][1])
+            for a, b in want.items():
+                if waited[q].get(a, 0) < b:
+                    Q[q].wait_ge(T.sem[a], b)
+                    waited[q][a] = b
+            o["fn"](T.sem[s])
+        for s, c in total.items():
+            g.wait_ge(T.sem[s], c)
+
+    def blk(t, j, n=1, w=K):
+        return t[:, j * w:(j + n) * w]
+
+    def ch(t, c):
+        return t[:, c * C:(c + 1) * C]
+
+    def cx(t, c):
+        return t[:, CH[c][0]:CH[c][1]]
+
+    def ks(n):
+        return ["%s.%d" % (n, c) for c in range(3)]
+
+    def bank(j):
+        return T["b%d" % j]
+
+    def compact(bk, j, z, zi, src, o, r):
+        pe([(blk(bank(bk), j), z[:, zi * 144 + 15 - i:zi * 144 + 143 - i], src[:, o + i:o + V:16], i == 0, i == 15)
+            for i in range(16)], r + ["zz"], ["#%d" % bk], V)
+
+    m = [T.m0, T.m1, T.m2]
+    yy = [T.yy0, T.yy1, T.yy2]
+    cc = [T.cc0, T.cc1, T.cc2]
+    hh = [T.hh0, T.hh1, T.hh2]
+    sp = [T.sp0, T.sp1]
+    ver = [T.ver0, T.ver1, T.ver2]
+    oh = [T.oh0, T.oh1]
+    rb = [T.rb0, T.rb1]
+    col = T.col
+    vv, vl, pv, wid, l1 = [blk(T.b5, j) for j in range(5)]
+    sw = T.cc0
+
+    def zb(t):
+        return 2 if t % 2 else 7
+
+    dma("s", T.curb[:], T.cur[:], [], ["cur", "~s"])
+    dma("a", T.dh[0, 128:256, :], T.s0[:, 0:NB], [], ["dh1", "~a"])
+    dma("s", T.dh[0, 0:128, :], T.s0[:, 0:NB], [], ["dh0", "~s"])
+    dma("a", ch(T.ptb, 0), ch(T.pt, 0), [], ["pt.0", "~a"], 0.65)
+    dma("s", ch(T.ptb, 1), ch(T.pt, 1), [], ["pt.1", "~s"], 0.65)
+    dma("a", ch(T.ptb, 2), ch(T.pt, 2), [], ["pt.2", "~a"], 0.65)
+    dma("s", sw[:, 0:V], T.s0[:], [], ["c0", "~s"], 1.0)
+
+    iota(T.pc[:, 0:2], [[0, 2]], 0, 1, ["pc"], False)
+    iota(T.gi[:], [[1, 8], [0, 16]], 0, -1, ["gi"])
+    iota(T.ci[:], [[1, 144]], 0, -1, ["ci"])
+    iota(T.lw[:], [[0, 8], [-2, 16]], 0, 0, ["lw"])
+    fill(T.one[:], 1.0, ["one"])
+    for c in range(3):
+        fill(T.vs[:, 3 * K + CH[c][0] // 16:3 * K + CH[c][1] // 16], float(WD[c]), ["vs3"])
+    ts(T.pc[:, 2:3], T.pc[:, 0:1], 15, None, OP.bitwise_and, None, ["pc"], ["pc2"])
+    ts(blk(T.mb, 4, 1, 128), T.gi[:], 0.0, None, OP.is_equal, None, ["gi"], ["le"])
+    cp(col[:, 0:1], T.pc[:, 2:3], ["pc2"], ["i"])
+    ts(T.pc[:, 3:4], T.pc[:, 0:1], 3, None, OP.bitwise_and, None, ["pc"], ["pc3"])
+    ts(col[:, 1:2], col[:, 0:1], -1.0, 15.0, OP.mult, OP.add, ["i"], ["c15"])
+    ts(col[:, 2:3], col[:, 0:1], col[:, 0:1], -1.0, OP.mult, OP.mult, ["i"], ["isq"])
+    ts(col[:, 4:5], col[:, 0:1], 1.5, None, OP.is_le, None, ["i"], ["wa"])
+    ts(col[:, 9:10], col[:, 0:1], float(K), None, OP.mult, None, ["i"], ["i96"])
+    for j in range(4):
+        ts(col[:, 5 + j:6 + j], T.pc[:, 3:4], float(j), None, OP.is_equal, None, ["pc3"], ["wq"])
+    ts(col[:, 3:4], col[:, 2:3], 1.0, None, OP.add, None, ["isq"], ["bias"])
+    ts(blk(T.mb, 0, 1, 128), T.ci[:, 0:128], 0.0, None, OP.is_equal, None, ["ci"], ["id"])
+    tt(blk(T.mb, 5, 1, 128), blk(T.mb, 4, 1, 128), T.lw[:], OP.mult, ["le", "lw"], ["lwm"])
+    ts(blk(T.zh, 0, 1, 144), T.ci[:], col[:, 1:2], None, OP.is_equal, None, ["ci", "c15"], ["zz"])
+    ts(blk(T.zb, 0, 1, 144), T.ci[:], col[:, 1:2], 0.5, OP.is_equal, OP.mult, ["ci", "c15"], ["zz"])
+    ts(blk(T.zb, 1, 1, 144), T.ci[:], col[:, 1:2], col[:, 4:5], OP.is_equal, OP.mult, ["ci", "c15", "wa"], ["zz"])
+    ts(blk(T.zb, 2, 1, 144), T.ci[:], col[:, 1:2], col[:, 0:1], OP.is_equal, OP.mult, ["ci", "c15", "i"], ["zz"])
+    sel(T.bd1[:], T.one[:], [[16, 8], [0, 16]], 15, -1, ["one"], ["bd1"])
+    iota(T.t4[:, 256:384], [[1, 128]], 255, -1, ["t4w"], False)
+    add("g", lambda s: spread(g, core, T, topo, rank, T.dh[0], sw, T.sem.as1, s), ["dh0", "dh1"], ["sent0.0"], 2.0, FAR + 1.5, newsem(nall))
+    arrives("c0.bus", "as1", 0, 0, 0.3)
+
+    ts(blk(T.ci2, 0), T.curb[:], 15, None, OP.bitwise_and, None, ["cur"], ["cs"])
+    ts(blk(T.ci2, 1), T.curb[:], 4, None, OP.arith_shift_right, None, ["cur"], ["ct"])
+    cp(blk(T.ft, 2, 2), T.ci2[:], ["cs", "ct"], ["f1"])
+    tt(blk(T.ft, 0, 2), T.ci2[:], T.ci2[:], OP.mult, ["cs", "ct"], ["f0"])
+    for f, q in ((2, "s"), (0, "a"), (3, "s"), (1, "a")):
+        dma(q, T.aq[0:8, f * V:(f + 1) * V], blk(T.ft, f), ["f%d" % (f // 2)], ["fw%d" % f, "aq%d" % f])
+    for j in range(4):
+        ts(blk(T.zh, 1 + j, 1, 144), T.ci[:], col[:, 1:2], col[:, 5 + j:6 + j], OP.is_equal, OP.mult, ["ci", "c15", "wq"], ["zz"])
+    sel(T.bd[:], T.bd1[:], [[-16, 8], [0, 16]], 0, 1, ["bd1"], ["bd"])
+    iota(T.t4[:, 0:128], [[0, 8], [1, 4], [0, 4]], 255, -1, ["t4a"], False)
+    iota(T.t4[:, 128:256], [[0, 8], [1, 4], [1, 4]], 256, -1, ["t4a"], False)
+    iota(blk(T.vs, 0), [[16, K]], 0, 0, ["vs"])
+    for c in range(3):
+        iota(T.vs[:, K + CH[c][0] // 16:K + CH[c][1] // 16], [[16, (CH[c][1] - CH[c][0]) // 16]], 0, 0, ["vs"])
+    iota(blk(T.vs, 2), [[1, K]], 0, 0, ["vs"])
+
+    def onehot(tb):
+        for c in range(3):
+            pe([(bank(c)[:], T.mb[0:8, 512:640], T.aq[0:8, tb * V + c * C:tb * V + (c + 1) * C], True, False),
+                (bank(c)[:], T.mb[0:8, 640:768], T.aq[0:8, (2 + tb) * V + c * C:(2 + tb) * V + (c + 1) * C], False, True)],
+               ["le", "lwm", "fw%d" % tb, "fw%d" % (2 + tb), "aq%d" % tb, "aq%d" % (2 + tb)], ["#%d" % c], 2 * C)
+            act(ch(oh[tb], c), bank(c)[:], AF.Relu, ["#%d" % c, "bias"], ["oh%d.%d" % (tb, c)], bias=col[:, 3:4], scale=-1.0, n=C)
+
+    def masked(out, on, tab, tn, mat, mn, tb):
+        for c in range(3):
+            bk = 3 + c % 2
+            pe([(bank(bk)[:], blk(T.mb, mat, 1, 128), ch(oh[tb], c), True, True)], [mn, "oh%d.%d" % (tb, c)], ["#%d" % bk], C)
+            tt(ch(out, c), ch(tab, c), bank(bk)[:], OP.mult, ["#%d" % bk, "%s.%d" % (tn, c)], ["%s.%d" % (on, c)], C)
+
+    def rows(k0, n):
+        act(blk(T.qh, k0, n), blk(T.qs, k0, n), AF.Identity, ["qs%d" % k0], ["qh%d" % k0], n=n * K)
+        tt(blk(T.ql, k0, n), blk(T.qs, k0, n), blk(T.qh, k0, n), OP.subtract, ["qs%d" % k0, "qh%d" % k0], ["ql%d" % k0], 2 * n * K)
+        for k in range(k0, k0 + n):
+            dma("s", T.aq[0:128:16, (4 + k) * V:(5 + k) * V], blk(T.qh, k), ["qh%d" % k0, "aq%d" % (4 + k)], ["aqh%d" % k])
+            dma("s", T.aq[1:128:16, (4 + k) * V:(5 + k) * V], blk(T.ql, k), ["ql%d" % k0, "aq%d" % (4 + k)], ["aql%d" % k])
+
+    def la(t, c):
+        j = 0 if t < 3 else t - 1
+        return T.la[:, j * K + CH[c][0] // 16:j * K + CH[c][1] // 16], "la%d" % (j + 1)
+
+    def product(t):
+        mt, n, u = m[t % 3], "m%d" % (t % 3), (t + 1) % 3
+        e = 1.0 if t % 2 else -1.0
+        if t > 1:
+            arrives(n + ".bus", "am%d" % t, 0, t - 1)
+        if t < 6:
+            dma("s", cc[u][:, 0:V], hh[t % 3][:], ks("h%d" % (t % 3)), ["c%d" % u], 1.0)
+        for c in range(3):
+            o, on = la(t, c)
+            tt(cx(T.pp, c), mt[:, 0:W].indirect(o), cx(T.mv, c), OP.mult, ks(n) + [n + ".bus", on, "mv.%d" % c], ["p.%d" % c], GA * WD[c])
+        for c in range(3):
+            if t < 6:
+                act(cx(m[u], c), cx(T.pp, c), AF.Abs, ["p.%d" % c] + ["y1.bus"] * (t == 1), ["m%d.%d" % (u, c)], bias=1.0, scale=-2.0, n=WD[c])
+                dma("s", cx(T.mv, c), cx(m[u], c), ["m%d.%d" % (u, c)], ["mv.%d" % c], WD[c] / 780)
+            if c == 0 and t < 6:
+                send(0, [cx(m[u], 0)], T.df, t, ["m%d.0" % u])
+            if c in SV.get(t, ()):
+                ts(cx(sp[t % 2], c), cx(T.pp, c), -2.0, 1.0, OP.mult, OP.add, ["p.%d" % c], ["sp%d.%d" % (t % 2, c)], WD[c])
+            else:
+                act(cx(sp[t % 2], c), cx(T.pp, c), AF.Identity, ["p.%d" % c], ["sp%d.%d" % (t % 2, c)], bias=1.0, scale=-2.0, n=WD[c])
+            if t == 6:
+                continue
+            act(cx(hh[u], c), cx(sp[t % 2], c), AF.Sign, ["sp%d.%d" % (t % 2, c)], ["h%d.%d" % (u, c)], bias=e * EPS, scale=e, n=WD[c])
+            if c == 0:
+                send(1, [cx(hh[t % 3], 0), cx(hh[u], 0)], T.dh, t, ["h%d.0" % (t % 3), "h%d.0" % u])
+        if t < 6:
+            dma("g", cc[u][:, 0:V], hh[u][:], ks("h%d" % u) + ["c%d" % u], ["c%d" % u], 2.0, accum_op=OP.add)
+
+    def drive(t):
+        yt, n = yy[t % 3], "y%d" % (t % 3)
+        if t > 1:
+            arrives(n + ".bus", "ay%d" % t, 2, t - 1)
+        for c in range(3):
+            o, on = la(t, c)
+            tt(cx(T.xx, c), yt[:, 0:W].indirect(o), cx(sp[t % 2], c), OP.mult,
+               ks(n) + [n + ".bus", on, "sp%d.%d" % (t % 2, c)], ["x.%d" % c], GA * WD[c])
+            act(blk(ver[c], 6 - t, 1, WD[c]), cx(T.xx, c), AF.Tanh, ["x.%d" % c], ["v%d.%d" % (t, c)], n=WD[c])
+
+    def blend(t, c, q="a"):
+        u, w = (t + 1) % 3, CH[c][1] - CH[c][0]
+        vs = ["v%d.%d" % (j, c) for j in range(1, t + 1)] + ["lb%d" % (t + 1)]
+        j = (2 * t - 1) * K
+        src = blk(ver[c], 5, 1, w) if t == 1 else ver[c][:, (6 - t) * w:6 * w].indirect(T.lb[:, j + CH[c][0] // 16:j + CH[c][1] // 16])
+        if t < 6:
+            act(cx(yy[u], c), src, AF.Identity, vs, ["y%d.%d" % (u, c)], bias=1.0, n=w * (GA if t > 1 else 1))
+            if c == 0:
+                send(2, [cx(yy[u], 0)], T.df, t, ["y%d.0" % u])
+        else:
+            if q == "a":
+                act(cx(T.pp, c), src, AF.Identity, vs, ["p.%d" % c], n=w * GA)
+            else:
+                cp(cx(T.pp, c), src, vs, ["p.%d" % c], w * GA)
+            dma("s", cx(T.y, c), cx(T.pp, c), ["p.%d" % c], [], w / 780)
+
+    def trigger(t):
+        n = "c%d" % (t % 3)
+        arrives(n + ".bus", "ac%d" % t, 1, t - 1)
+        for c in range(2):
+            a, b = c * V // 2, (c + 1) * V // 2
+            tt(T.zp[:, a:b], cc[t % 3][:, 0:W].indirect(T.lb[:, (2 * t - 4) * K + a // 16:(2 * t - 4) * K + b // 16]),
+               hh[t % 3][:, a:b], OP.mult, [n, n + ".bus", "lb%d" % t] + ks("h%d" % (t % 3)), ["zp"], GA * V / 2)
+        compact(zb(t), 0, T.zb, 0, T.zp, 0, ["zp"])
+
+    def fold():
+        for c in range(3):
+            bk = 3 + c % 2
+            pe([(bank(bk)[:], T.mh[:], ch(rb[1], c), True, True)], ["fk", "rb1.%d" % c], ["#%d" % bk], C)
+            tt(ch(T.ra, c), ch(T.aq, c), bank(bk)[:], OP.mult, ["#%d" % bk, "o4.%d" % c], ["ra.%d" % c], C)
+        for j in range(4):
+            compact(1, j, T.zh, 1 + j, T.ra, 0, ks("ra"))
+        act(blk(T.qt, 1, 4), blk(bank(1), 0, 4), AF.Identity, ["#1"], ["qt1"], bias=1024.0, n=4 * K)
+
+    def ahead(t):
+        if t == 2:
+            cp(blk(T.ti, 1), T.c1[:], ["cur1"], ["ri"])
+        else:
+            tt(blk(T.ti, 1), T.c1[:], blk(T.jj, 0), OP.add, ["cur1", "j"], ["ri"], 2 * K)
+        ts(T.rr[:], blk(T.ti, 1), 3, None, OP.bitwise_and, None, ["ri"], ["rr"])
+        ts(T.nx[:], T.rr[:], float(V), float(V * (t - 1)), OP.mult, OP.add, ["rr"], ["nx"])
+        tt(T.nx2[:], T.nx[:], pv, OP.add, ["nx", "vv"], ["nx2"])
+
+    def masks(t):
+        b, k = bank(zb(t)), "#%d" % zb(t)
+        if t < 6:
+            tt(blk(b, 1), blk(b, 0), T.thr[:], OP.is_gt, [k, "thr"], ["k1%d" % t])
+        ts(blk(b, 2), blk(b, 0), 2.5, None, OP.is_ge, None, [k], ["k3%d" % t])
+        ts(blk(b, 3), blk(b, 0), -1.5, None, OP.is_le, None, [k], ["kh%d" % t])
+
+    def held(t):
+        tt(T.be[:], blk(bank(zb(t)), 3), blk(T.vs, 3) if t == 2 else T.bp[:], OP.mult,
+           ["#%d" % zb(t), "kh%d" % t, "vs3", "bp"], ["be"])
+
+    def elect(t):
+        b, k, k1, k3, kh = bank(zb(t)), "#%d" % zb(t), "k1%d" % t, "k3%d" % t, "kh%d" % t
+        pb = blk(b, 4)
+        tt(T.pr[:], blk(b, 1, 2), T.dd[:], OP.mult, [k, k1, k3, "d1", "d3"], ["pr"], 2 * K)
+        held(t)
+        tt(l1, blk(T.pr, 0), pv if t == 2 else vv, OP.add, ["pr", "vv"], ["l1"])
+        tt(pb, blk(b, 3), blk(T.dt, 0) if t == 2 else T.db[:], OP.mult, [k, kh, "db", "dt0"], ["pb"])
+        tt(T.l2[:], l1, blk(T.pr, 1), OP.add, ["l1", "pr"], ["l2"])
+        tt(blk(T.bs, 1), T.be[:], vl, OP.add, ["be", "vv"], ["yl"])
+        cp(T.ll[:], T.l2[:], ["l2"], ["ll"])
+        a0 = 6 - t
+        act(blk(T.aq, a0 - 1, 1, V), T.aq[:, a0 * V:9 * V].indirect(T.ll[:]), AF.Identity,
+            ["ll"] + ["aq%d" % j for j in range(a0, 9)] + ["aq%s%d" % (x, j) for x in "hl" for j in range(5)],
+            ["aq%d" % (a0 - 1)], n=GA * V)
+        compact(6, 0, T.zb, 1, T.aq, (a0 - 1) * V, ["aq%d" % (a0 - 1)])
+        tt(blk(T.bs, 0), pb, blk(T.qt, 0) if t == 2 else blk(T.bs, 0), OP.add, [k, "pb", "b", "qt0"], ["b"])
+        if t == 2:
+            cp(T.jj[:], blk(b, 2, 2), [k, k3, kh], ["j"], 2 * K)
+        else:
+            tt(T.jj[:], T.jj[:], blk(b, 2, 2), OP.add, [k, k3, kh, "j"], ["j"], 2 * K)
+        cp(blk(T.lb, 2 * t - 2, 2), T.bs[:], ["b", "yl"], ["lb%d" % (t + 1)], 2 * K)
+
+    def prepare(t):
+        a, n = blk(bank(6), 0), t - 2
+        tt(T.bp[:], T.be[:], wid, OP.add, ["be", "vv"], ["bp"])
+        if t == 6:
+            return
+        ahead(t)
+        for k in range(n):
+            ts(blk(T.b4, k), blk(T.jj, 1), k + 0.5, None, OP.is_ge, None, ["j"], ["#4"])
+        tt(blk(T.b3, 0, n), blk(T.b4, 0, n), blk(T.f2, 0, n), OP.mult, ["#4", "f2"], ["#3"], n * K)
+        ts(T.thr[:], a, V - 0.5, 2.0, OP.is_ge, OP.mult, ["#6"], ["thr"])
+        tt(blk(T.dd, 0), a, blk(T.vs, 0), OP.subtract, ["#6", "vv"], ["d1"])
+        acc, an = blk(T.dt, 0), "dt0"
+        for k in range(n):
+            out, on = (T.db[:], "db") if k == n - 1 else (blk(T.ga, k), "ga%d" % k)
+            tt(out, acc, blk(T.b3, k), OP.add, [an, "#3"], [on])
+            acc, an = out, on
+            if k == 0:
+                tt(blk(T.dd, 1), T.nx2[:], a, OP.subtract, ["#6", "nx2"], ["d3"])
+
+    onehot(0)
+    for c in range(3):
+        ts(ch(T.si, c % 2), ch(T.ptb, c), 4095, None, OP.bitwise_and, None, ["pt.%d" % c, "sf.%d" % (c - 2)], ["si.%d" % c], C)
+        ts(ch(T.sf, c), ch(T.si, c % 2), -1024.0, None, OP.add, None, ["si.%d" % c], ["sf.%d" % c], C)
+    ts(T.t4[:, 256:384], T.t4[:, 256:384], 12, None, OP.bitwise_and, None, ["t4w"], ["t4w"], 128)
+    ts(T.t4[:, 0:256], T.t4[:, 0:256], 3, None, OP.bitwise_and, None, ["t4a"], ["t4a"], 256)
+    ts(T.e4[:], T.t4[:], 0.0, None, OP.is_equal, None, ["t4w", "t4a"], ["e4"], 384)
+    masked(T.ra, "ra", T.sf, "sf", 0, "id", 0)
+    compact(6, 0, T.zh, 0, T.ra, 0, ks("ra"))
+    for c in range(3):
+        act(cx(m[1], c), cx(sw, c), AF.Abs, ["c0"], ["m1.%d" % c], n=WD[c])
+        dma("s", cx(T.mv, c), cx(m[1], c), ["m1.%d" % c], ["mv.%d" % c], WD[c] / 780)
+        act(cx(hh[1], c), cx(sw, c), AF.Sign, ["c0"], ["h1.%d" % c], bias=-EPS, scale=-1.0, n=WD[c])
+        act(cx(yy[1], c), cx(sw, c), AF.Identity, ["c0"], ["y1.%d" % c], bias=1.0, n=WD[c])
+    for j in range(4, 9):
+        dma("s", blk(T.aq, j, 1, V), T.s0[:], ks("mv"), ["aq%d" % j], 1.0)
+    act(m[1][:, V:W], sw[:, V:W], AF.Abs, ["c0.bus"], ["m1.bus"], n=W - V)
+    act(yy[1][:, V:W], sw[:, V:W], AF.Identity, ["c0.bus"], ["y1.bus"], bias=1.0, n=W - V)
+    onehot(1)
+    tt(blk(T.mb, 1, 1, 128), T.e4[:, 256:384], T.bd[:], OP.mult, ["e4", "bd"], ["w4"], 256)
+    tt(blk(T.mb, 2, 1, 128), T.e4[:, 0:128], T.bd[:], OP.mult, ["e4", "bd"], ["o4m"], 256)
+    tt(T.mh[:], T.e4[:, 128:256], T.bd[:], OP.mult, ["e4", "bd"], ["fk"], 256)
+    for c in range(3):
+        ts(ch(T.ptb, c), ch(T.ptb, c), 2.0 ** -12, -1024.25, OP.mult, OP.add, ["pt.%d" % c, "si.%d" % c], ["ti.%d" % c], C)
+    ts(blk(T.la, 0), blk(bank(6), 0), 1024.0, None, OP.add, None, ["#6"], ["la1"])
+    act(blk(T.qs, 0), blk(bank(6), 0), AF.Identity, ["#6"], ["qs0"], bias=1024.0)
+
+    product(1)
+    masked(rb[0], "rb0", T.sf, "sf", 1, "w4", 0)
+    drive(1)
+    for c in range(3):
+        blend(1, c)
+    compact(7, 0, T.zb, 2, oh[0], 0, ks("oh0"))
+    compact(7, 1, T.zb, 2, oh[1], 0, ks("oh1"))
+    act(T.c0[:], blk(bank(7), 0, 2), AF.Identity, ["#7"], ["cur0"], n=2 * K)
+    act(T.c1[:], blk(bank(7), 0), AF.Identity, ["#7"], ["cur1"], bias=1.0)
+    for j in range(4):
+        compact(0, j, T.zh, 1 + j, rb[0], 0, ks("rb0"))
+    act(blk(T.qs, 1, 4), blk(bank(0), 0, 4), AF.Identity, ["#0"], ["qs1"], bias=1024.0, n=4 * K)
+    rows(1, 4)
+    masked(rb[1], "rb1", T.ptb, "ti", 1, "w4", 1)
+    for c in range(3):
+        bk = 1 + c % 2
+        pe([(bank(bk)[:], blk(T.mb, 2, 1, 128), ch(oh[1], c), True, True)], ["o4m", "oh1.%d" % c], ["#%d" % bk], C)
+        act(ch(T.aq, c), bank(bk)[:], AF.Identity, ["#%d" % bk], ["o4.%d" % c, "aq0"], n=C)
+    masked(T.ra, "ra", T.ptb, "ti", 0, "id", 1)
+    compact(6, 1, T.zh, 0, T.ra, 0, ks("ra"))
+    rows(0, 1)
+    ts(blk(T.vs, 0, 2), blk(T.vs, 0, 2), col[:, 0:1], None, OP.add, None, ["vs", "i"], ["vs0"])
+    ts(pv, blk(T.vs, 2), col[:, 9:10], None, OP.add, None, ["vs", "i96"], ["vv"])
+    cp(wid, blk(T.vs, 3), ["vs3"], ["vv"])
+    cp(blk(T.b5, 0, 2), blk(T.vs, 0, 2), ["vs0"], ["vv"])
+    cp(blk(T.ti, 0), blk(T.qs, 0), ["qs0"], ["ai"])
+    ts(blk(T.lb, 0), blk(bank(6), 1), 1024.0, None, OP.add, None, ["#6"], ["lb2"])
+    act(blk(T.qt, 0), blk(bank(6), 1), AF.Identity, ["#6"], ["qt0"], bias=1024.0)
+    fold()
+    ahead(2)
+    ts(blk(T.tj, 0), blk(T.ti, 0), 15, None, OP.bitwise_and, None, ["ai"], ["alo"])
+    ts(blk(T.tj, 1), blk(T.ti, 0), 4, None, OP.arith_shift_right, None, ["ai"], ["ahi"])
+    ts(T.thr[:], blk(T.qs, 0), V - 0.5, 2.0, OP.is_ge, OP.mult, ["qs0"], ["thr"])
+    ts(l1, blk(T.tj, 0), float(K), None, OP.mult, None, ["alo"], ["l1"])
+    tt(T.pa[:], l1, blk(T.tj, 1), OP.add, ["l1", "ahi"], ["pa"])
+
+    for t in range(2, 6):
+        product(t)
+        trigger(t)
+        if t == 2:
+            tt(blk(T.dd, 0), T.pa[:], pv, OP.subtract, ["pa", "vv"], ["d1"])
+            tt(blk(T.dd, 1), T.nx2[:], T.pa[:], OP.subtract, ["pa", "nx2"], ["d3"], 2 * K)
+            tt(blk(T.dt, 0), blk(T.qt, 1), blk(T.qt, 0), OP.subtract, ["qt0", "qt1"], ["dt0"], 2 * K)
+        else:
+            prepare(t)
+        masks(t)
+        elect(t)
+        drive(t)
+        for c in range(3):
+            blend(t, c)
+        if t == 2:
+            tt(blk(T.b3, 0, 3), blk(T.qt, 2, 3), blk(T.qt, 1, 3), OP.subtract, ["qt1"], ["#3"], 6 * K)
+            tt(blk(T.f2, 0), blk(T.b3, 0), blk(T.dt, 0), OP.subtract, ["dt0", "#3"], ["f2"])
+            cp(blk(T.dt, 1, 2), blk(T.b3, 0, 2), ["#3"], ["dt1"], 2 * K)
+            tt(blk(T.f2, 1, 2), blk(T.b3, 1, 2), blk(T.dt, 1, 2), OP.subtract, ["dt1", "#3"], ["f2"], 2 * K)
+        cp(blk(T.la, t), blk(bank(6), 0), ["#6"], ["la%d" % (t + 1)])
+    product(6)
+    trigger(6)
+    prepare(6)
+    tt(T.ti[:], T.c0[:], T.jj[:], OP.add, ["cur0", "j"], ["ai", "ri"], 4 * K)
+    drive(6)
+    ts(T.tj[:], T.ti[:], 15, None, OP.bitwise_and, None, ["ai"], ["alo", "ahi"], 2 * K)
+    masks(6)
+    ts(T.tf[:], T.tj[:], 15.0, -16.0, OP.is_equal, OP.mult, ["alo"], ["tf"])
+    held(6)
+    ts(T.dd[:], T.tf[:], 1.0, None, OP.add, None, ["tf"], ["d1", "d3"])
+    tt(blk(T.bs, 1), T.be[:], vl, OP.add, ["be", "vv"], ["yl"])
+    tt(T.pr[:], blk(T.b7, 2, 2), T.dd[:], OP.mult, ["#7", "k36", "kh6", "d1"], ["pr"], 2 * K)
+    cp(blk(T.lb, 11), blk(T.bs, 1), ["yl"], ["lb7"])
+    tt(T.qq[:], T.pr[:], T.tj[:], OP.add, ["pr", "alo"], ["qq"], 4 * K)
+    blend(6, 0, "v")
+    ts(l1, blk(T.qq, 1), 16.0, None, OP.mult, None, ["qq"], ["l1"])
+    tt(T.qb[:], l1, blk(T.qq, 0), OP.add, ["qq", "l1"], ["qb"])
+    for c in range(3):
+        pe([(bank(c)[0:8, i:C:16], T.mb[:, i:128:16], T.qb[:, 32 * c:32 * c + 32], True, True) for i in range(16)],
+           ["id", "qb"], ["#%d" % c], C)
+    blend(6, 1)
+    blend(6, 2, "v")
+    act(T.mv[0:8, 0:C], bank(0)[0:8, :], AF.Identity, ["#0"] + ks("sp0"), ["q0"], n=C)
+    act(T.mv[0:8, C:2 * C], bank(1)[0:8, :], AF.Identity, ["#1"] + ks("sp0"), ["q1"], n=C)
+    cp(T.mv[0:8, 2 * C:V], bank(2)[0:8, :], ["#2"] + ks("sp0"), ["q2"], C)
+    dma("s", T.q[:], T.mv[0:8, :], ["q0", "q1", "q2"], [])
+    issue()

@@ -5,14 +5,27 @@ from concourse.mybir import AluOpType as OP, ActivationFunctionType as AF
 V, NB, W, C, K = 1536, 192, 2112, 512, 96
 SH = {1: 1, 2: 3, 3: 6}
 CH = [(0, 192), (192, 864), (864, 1536)]
-SV = {}
-EPS = 2.0 ** -26
-CYC, PEC, GA, DMA, FAR, HOP, SOON = 0.0009, 0.6, 1.56, 2.0, 4.5, 0.12, 0.25
-FIX = {"v": 0.04, "a": 0.1, "p": 0.1, "g": 0.15}
-SELF, TRIES = 0.08, 6000
-CASES = [(1.56, 1.0, 1.0), (1.15, 1.2, 0.7), (2.0, 0.75, 1.4)]
 WD = [b - a for a, b in CH]
-ORDER = []
+HALF = [(0, NB), (NB, V)]
+SO, AY = W, W + 4 * V
+DK = 6 * K
+EPS = 2.0 ** -26
+EV = {t: (2,) for t in range(2, 6)}
+CYC, PEC, GA, DMA, FAR, HOP, SELF = 0.00083, 0.6, 1.56, 2.0, 3.9, 0.12, 0.08
+FIX = {"v": 0.03, "a": 0.06, "p": 0.1, "g": 0.15}
+CASES = [(1.1, 1.15, 1.15, 1.15, 1.8), (1.45, 1.55, 1.0, 1.5, 1.0), (1.0, 1.45, 0.95, 1.0, 1.0)]
+SEED, MOVES, HEAT, SOFT = 1, 70000, 0.05, 0.1
+EARLY = dict.fromkeys("vapx", 30.0) | {"g": 1.5, "s": 2.5}
+PERIOD = 8.6
+START = {t: 10.0 + (t - 1) * PERIOD + (t > 1) * 1.2 for t in range(1, 7)}
+PLAN = {"g1": (0.0, 2.1, 2.85), "g2": (1.85, 0.3, 1.05), "k": (3.7, 3.6), "e2": (0.4, 4.2, 5.5), "e3": (0.65, 2.9, 3.6),
+        "e1": (0.9, 6.1, 5.2), "el": (4.6, 5.2, 6.7, 9.6), "keep": (4.3,), "turn": (4.1, 6.5), "g3": (4.0, 7.1, 5.8),
+        "e4": (4.85, 10.3, 9.5), "add": (4.3,)}
+FIRST = dict(PLAN, g1=(0.0, 1.6, 2.3), e2=(0.4, 2.5, 3.7), e3=(0.7, 3.1, 4.3), e1=(2.0, 5.8, 6.4), g3=(3.0, 6.4, 7.1),
+             e4=(3.6, 8.8, 12.8), add=(5.0,))
+LAST = dict(PLAN, g2=(1.0, -0.5, 0.25), g1=(2.8, 1.3, 2.0), k=(2.3, 2.2), keep=(2.4,), e1=(3.2, 2.1, 2.8), g3=(5.4, 3.9, 4.65),
+            e4=(6.3, 4.7, 5.5))
+ORDER, SCORE = [], []
 F, B, H, I, U = "float32", "bfloat16", "float16", "int32", "uint16"
 
 
@@ -21,59 +34,56 @@ def sb(n, d):
 
 
 SCRATCH = {
-    "ptb": sb(V, I), "si": sb(2 * C, I), "sf": sb(V, H), "oh0": sb(V, B), "oh1": sb(V, B),
-    "ra": sb(V, H), "rb0": sb(V, H), "rb1": sb(V, H),
-    "pp": sb(V, F), "xx": sb(V, F), "zp": sb(V, B), "aq": sb(9 * V, B), "mv": sb(V, F),
+    "ptb": sb(V, I), "si": sb(2 * C, I), "sf": sb(V, H), "oh1": sb(V, B),
+    "ra": sb(V, H), "rb0": sb(V, H), "rb1": sb(V, H), "rt": sb(V, H), "fw": sb(2 * V, B),
+    "pp": sb(V, F), "mv": sb(V, F), "zp": sb(V, B), "aq": sb(AY + W, B), "th": sb(W - V, B), "sg": sb(3 * NB, B),
     "sp0": sb(V, F), "sp1": sb(V, F),
-    "t4": sb(384, I), "e4": sb(384, F), "one": sb(128, F), "bd1": sb(128, F), "bd": sb(128, F), "c1": sb(K, F), "rr": sb(K, I),
-    "ci": sb(144, F), "gi": sb(128, F), "lw": sb(128, F), "pc": sb(4, I), "col": sb(16, F),
-    "zb": sb(3 * 144, B), "zh": sb(5 * 144, H), "mb": sb(6 * 128, B), "mh": sb(128, H),
-    "curb": sb(K, I), "ci2": sb(2 * K, I), "ft": sb(4 * K, B),
-    "vs": sb(4 * K, F), "qs": sb(5 * K, F), "qt": sb(5 * K, F),
-    "qh": sb(5 * K, B), "ql": sb(5 * K, B), "c0": sb(2 * K, F), "ti": sb(2 * K, I), "tj": sb(2 * K, I),
-    "tf": sb(2 * K, F), "pa": sb(K, F), "thr": sb(K, F), "dd": sb(2 * K, F), "pr": sb(2 * K, F),
-    "l2": sb(K, F), "nx": sb(K, F), "nx2": sb(K, F), "jj": sb(2 * K, F), "bs": sb(2 * K, F),
-    "be": sb(K, F), "bp": sb(K, F), "dt": sb(4 * K, F), "f2": sb(3 * K, F), "db": sb(K, F),
-    "ga": sb(2 * K, F), "qq": sb(2 * K, F), "qb": sb(K, B),
-    "la": sb(6 * K, U), "ll": sb(K, U), "lb": sb(12 * K, U),
-    "df": ("dram", [6, 256, NB], F), "dh": ("dram", [7, 256, NB], B),
+    "t4": sb(384, I), "e4": sb(384, F), "one": sb(128, F), "bd1": sb(128, F), "bd": sb(128, F),
+    "ci": sb(144, B), "gi": sb(128, F), "lw": sb(128, F), "pc": sb(6, I), "col": sb(16, F),
+    "zb": sb(4 * 144, B), "zh": sb(9 * 144, H), "mb": sb(11 * 128, B), "mh": sb(128, H), "ih": sb(128, H),
+    "curb": sb(K, I), "ci2": sb(2 * K, I), "ft": sb(4 * K, B), "vs": sb(4 * K, F),
+    "kb": sb(10 * K, B), "kh": sb(K, H), "qh": sb(5 * K, B), "ql": sb(5 * K, B),
+    "dk": sb(5 * DK, B), "dt": sb(5 * K, B), "so": sb(4 * K, F), "yo": sb(2 * K, F), "to": sb(5 * K, F),
+    "wq": sb(2 * K, B), "qb": sb(2 * K, B),
+    "la": sb(6 * K, U), "ll": sb(K, U), "lb": sb(5 * K, U), "ly": sb(5 * K, U),
+    "df": ("dram", [11, 256, NB], F), "dh": ("dram", [7, 256, NB], B),
 }
 for _j in range(3):
     SCRATCH["m%d" % _j] = sb(W, F)
     SCRATCH["yy%d" % _j] = sb(W, F)
-    SCRATCH["cc%d" % _j] = sb(W, B)
-    SCRATCH["hh%d" % _j] = sb(V, B)
-    SCRATCH["ver%d" % _j] = sb(6 * (CH[_j][1] - CH[_j][0]), F)
+    SCRATCH["hh%d" % _j] = sb(W, B)
+    SCRATCH["xv%d" % _j] = sb(6 * WD[_j], F)
 for _j in range(8):
     SCRATCH["b%d" % _j] = ("psum", [128, C], F)
 
-SEMAPHORES = (["ev", "ea", "ep", "eg", "out", "as1"] + ["hin%d" % t for t in range(2, 7)]
-              + ["a%s%d" % (k, t) for k in "mcy" for t in range(2, 7)] + ["d%d" % j for j in range(95)])
-
-
-def helpers(core, T, topo):
-    return [c for c in topo.cores_of(core) if topo.die(c) == topo.die(core) and T.rank_of(c) is None][:3]
+HANDS = [[("y", 1)] + [(k, t) for t in range(2, 7) for k in "my"], [("c", t) for t in range(2, 7)]]
+SEMAPHORES = (["ev", "ea", "ep", "eg", "as1", "out"] + [x + k + str(t) for h in HANDS for k, t in h for x in "ha"]
+              + ["d%d" % j for j in range(90)])
 
 
 def mask_of(engines):
     return sum(1 << e for e in engines)
 
 
-def spread(g, core, T, topo, rank, stage, window, sem, local):
+def apart(T, topo, rank):
+    return [d for d in SH if T.cores[(rank + d) % len(T.cores)] not in topo.cores_of(T.cores[rank])]
+
+
+def spread(g, core, T, topo, rank, stage, window, sem, local, back=None, ds=SH):
     n = len(T.cores)
-    dst = {d: T.cores[(rank + d) % n] for d in SH}
-    narrow = min((topo.engines(core, dst[d]) for d in SH), key=len)
-    far = [d for d in SH if len(topo.engines(core, dst[d])) == len(narrow)]
+    dst = {d: T.cores[(rank + d) % n] for d in [0] * (back is not None) + list(ds)}
+    far = [d for d in dst if dst[d] not in topo.cores_of(core)]
+    narrow = topo.engines(core, dst[far[0]]) if far else []
     trs, sent = [], 0
-    for d in SH:
-        if d in far:
-            q = far.index(d)
-            eng = narrow[q * len(narrow) // len(far):(q + 1) * len(narrow) // len(far)]
-        else:
-            eng = [e for e in topo.engines(core, dst[d]) if e not in narrow]
+    for d in dst:
+        kin = far if d in far else [x for x in dst if x not in far]
+        pool = narrow if d in far else [e for e in topo.engines(core, dst[d]) if e not in narrow]
+        q = kin.index(d)
+        eng = pool[q * len(pool) // len(kin):(q + 1) * len(pool) // len(kin)]
         rid, pid = topo.addr(dst[d], core)
+        row, o = (16 * SH[d], V + (d - 1) * NB) if d else (0, 0)
         trs.append(RemoteDMATransfer(dst_ids=[DstId(rid=rid, pnc=pid)], dma_engine_mask=mask_of(eng), remote_sem=sem,
-                                     src=stage[16 * SH[d]:16 * SH[d] + 128, :], dst=window[:, V + (d - 1) * NB:V + d * NB]))
+                                     src=stage[row:row + 128, :], dst=(window if d else back)[:, o:o + NB]))
         sent += len(eng)
     g.remote_dma_fused(trs, local_sem=local)
     return sent
@@ -88,86 +98,159 @@ def arrange(ops):
         for j, hard in deps[i]:
             kids[j].append((i, hard))
 
-    def costs(ga, dm, pc):
+    def costs(cf, ga, dm, pc, lk):
         busy, lat = [], []
         for o in ops:
-            f = ga / GA if o["gather"] else pc if o["q"] == "p" else 1.0
+            f = cf * ga / GA if o["gather"] else pc if o["q"] == "p" else 1.0 if o["sem"] else cf
             busy.append(o["busy"] * f)
-            lat.append(o["lat"] * (dm if o["sem"] else f))
-        return busy, lat
+            lat.append(o["lat"] * (dm if o["sem"] else f) + o["port"] * (lk - 1))
+        return busy, lat, [o["port"] * lk for o in ops]
 
     cases = [costs(*c) for c in CASES]
-
     move = [o["move"] for o in ops]
     firm = [[(j, HOP if qs[j] != qs[i] else SELF) for j, hard in deps[i] if hard] for i in range(n)]
+    start, tight = [0.0] * n, []
 
     def ends(seq):
         out = 0.0
-        for busy, lat in cases:
-            free, done, pipe = dict.fromkeys("vapgsx", 0.0), [0.0] * n, 0.0
+        for busy, lat, port in cases:
+            free, done, pipe, link = dict.fromkeys("vapgsx", 0.0), [0.0] * n, 0.0, 0.0
             for i in seq:
                 t = free[qs[i]]
                 for j, gap in firm[i]:
                     if done[j] + gap > t:
                         t = done[j] + gap
+                start[i] = t
                 free[qs[i]] = t + busy[i]
                 done[i] = t + lat[i]
                 if move[i]:
                     pipe = max(pipe + move[i], done[i])
                     done[i] = pipe
-            out += max(done)
+                elif port[i]:
+                    link = max(link + port[i], done[i])
+                    done[i] = link
+            out += max(done) + SOFT * sum(done) / n
         return out / len(cases)
 
-    def build(bonus, case):
-        busy, lat = case
-        rest = list(lat)
-        for i in range(n - 1, -1, -1):
-            rest[i] += bonus[i]
-            for j, hard in deps[i]:
-                rest[j] = max(rest[j], lat[j] + HOP + rest[i])
+    def longest(seq):
+        pairs = []
+        for busy, lat, port in cases:
+            free, done, why, prev = dict.fromkeys("vapgsx", 0.0), [0.0] * n, [None] * n, {}
+            for i in seq:
+                t, why[i] = free[qs[i]], (prev.get(qs[i]), True)
+                for j, gap in firm[i]:
+                    if done[j] + gap > t:
+                        t, why[i] = done[j] + gap, (j, False)
+                free[qs[i]], done[i], prev[qs[i]] = t + busy[i], t + lat[i], i
+            i = max(range(n), key=lambda k: done[k])
+            while why[i][0] is not None:
+                if why[i][1]:
+                    pairs.append((why[i][0], i))
+                i = why[i][0]
+        return pairs
+
+    def moved(seq):
+        step = 1 if rng.randint(0, 2) else -1
+        if tight and rng.randint(0, 3):
+            a = seq.index(tight[int(rng.randint(0, len(tight)))][step < 0])
+        else:
+            a = int(rng.randint(0, n))
+        i = seq[a]
+        skip, b = int(rng.randint(1, 4)), a
+        near = set(k for k, hard in (kids[i] if step > 0 else deps[i]))
+        while skip:
+            b += step
+            if b < 0 or b >= n:
+                return None
+            skip -= qs[seq[b]] == qs[i]
+        lo, hi = min(a, b), max(a, b)
+        along, stay = [i], []
+        for j in (seq[a + 1:hi + 1] if step > 0 else seq[lo:a][::-1]):
+            if j in near:
+                along.append(j)
+                near.update(k for k, hard in (kids[j] if step > 0 else deps[j]))
+            else:
+                stay.append(j)
+        if seq[b] in along:
+            return None
+        mid = stay + along if step > 0 else along[::-1] + stay[::-1]
+        return seq[:lo] + mid + seq[hi + 1:]
+
+    due = [o["due"] for o in ops]
+    for i in range(n - 1, -1, -1):
+        for j, hard in deps[i]:
+            due[j] = min(due[j], due[i])
+
+    def first(case, soon):
+        busy, lat, port = case
         need, ready, free = [len(d) for d in deps], [0.0] * n, dict.fromkeys("vapgsx", 0.0)
-        cand, seq, pipe = {q: [] for q in free}, [], 0.0
+        cand, seq, pipe, link = {q: [] for q in free}, [], 0.0, 0.0
         for i in range(n):
             if not need[i]:
                 cand[qs[i]].append(i)
         while len(seq) < n:
-            t0, q = min((max(free[q], min(ready[i] for i in c)), q) for q, c in cand.items() if c)
-            i = max((j for j in cand[q] if ready[j] <= t0 + SOON), key=lambda j: (rest[j] - 2 * max(0.0, ready[j] - t0), -j))
+            t0, q = min((max(free[q], min(max(ready[i], due[i] - EARLY[q]) for i in c)), q) for q, c in cand.items() if c)
+            i = min((j for j in cand[q] if max(ready[j] - soon, due[j] - EARLY[q]) <= t0), key=lambda j: (due[j], j))
             cand[q].remove(i)
             seq.append(i)
-            t = max(t0, ready[i])
-            free[q] = t + busy[i]
-            done = t + lat[i]
+            t = max(free[q], ready[i])
+            free[q], done = t + busy[i], t + lat[i]
             if move[i]:
                 pipe = done = max(pipe + move[i], done)
+            elif port[i]:
+                link = done = max(link + port[i], done)
             for k, hard in kids[i]:
-                ready[k] = max(ready[k], done + (HOP if qs[k] != q else SELF) if hard else t + busy[i])
+                ready[k] = max(ready[k], done + (HOP if qs[k] != q else SELF) if hard else t)
                 need[k] -= 1
                 if not need[k]:
                     cand[qs[k]].append(k)
         return seq
 
-    rng = np.random.RandomState(1)
-    bonus = [0.0] * n
-    best = build(bonus, cases[0])
-    score = ends(best)
-    for it in range(TRIES):
-        trial = list(bonus)
-        for i in rng.randint(0, n, 6):
-            trial[i] = max(0.0, trial[i] + float(rng.normal()) * 2.5)
-        seq = build(trial, cases[0])
+    cur = best = min((first(c, s) for c in cases for s in (0.15, 0.3, 0.5, 0.8)), key=ends)
+    now = score = ends(best)
+    SCORE.append(score)
+    rng = np.random.RandomState(SEED)
+    for it in range(MOVES):
+        if it % 100 == 0:
+            ends(cur)
+            cur = sorted(cur, key=lambda i: start[i])
+            now = ends(cur)
+        if it % 20 == 0:
+            tight[:] = longest(cur)
+        seq = moved(cur)
+        if seq is None:
+            continue
         s = ends(seq)
-        if s <= score:
-            bonus, best, score = trial, seq, s
+        if s <= now + HEAT * (1 - it / MOVES) * rng.exponential():
+            cur, now = seq, s
+            if s < score:
+                best, score = seq, s
+    SCORE.append(score)
     return best
+
+
+def helpers(core, T, topo):
+    return [c for c in topo.cores_of(core) if topo.die(c) == topo.die(core) and T.rank_of(c) is None][:3]
+
+
+def feed(T, topo, rank, j):
+    core = T.cores[rank]
+    e = topo.engines(core, helpers(core, T, topo)[j])
+    return e if j == 2 else e[j * len(e) // 2:(j + 1) * len(e) // 2]
+
+
+def staged(T, k, t):
+    return T.dh[t - 1] if k == "c" else T.df[t - 1 + 5 * (k == "m")]
 
 
 def helper_program(g, core, T, topo, rank, j):
     sent = 0
-    for t in range(2, 7):
-        g.wait_ge(T.sem["hin%d" % t], 2 * len(topo.engines(T.cores[rank], core)))
-        sent += spread(g, core, T, topo, rank, (T.dh if j == 1 else T.df)[t - 1], T["%s%d" % (("m", "cc", "yy")[j], t % 3)],
-                       T.sem["a%s%d" % ("mcy"[j], t)], T.sem.out)
+    far = apart(T, topo, rank)
+    for k, t in HANDS[j == 2]:
+        g.wait_ge(T.sem["h%s%d" % (k, t)], 2 * len(feed(T, topo, rank, j)))
+        win = T["hh%d" % ((t - 1) % 3)] if k == "c" else T["%s%d" % ("m" if k == "m" else "yy", t % 3)]
+        sent += spread(g, core, T, topo, rank, staged(T, k, t), win, T.sem["a%s%d" % (k, t)], T.sem.out,
+                       [None, T.mv if k == "m" else None, win][j], [[d for d in SH if d != far[1]], far[1:], SH][j])
     g.wait_ge(T.sem.out, sent)
 
 
@@ -182,9 +265,12 @@ def rank_program(g, core, T, topo):
     hs = helpers(core, T, topo)
     nall = max(len(topo.engines(core, c)) for c in T.cores if c != core)
     Q = {"v": g.vector, "a": g.scalar, "p": g.tensor, "g": g, "s": g.sync}
-    ops, last, readers, nd = [], {}, {}, [0]
+    ops, last, readers, nd, due = [], {}, {}, [0], [0.0]
 
-    def add(q, fn, r, w, busy, lat, sem=None, move=0.0):
+    def at(t, k=None, c=0):
+        due[0] = t if k is None else START[t] + (FIRST if t == 1 else LAST if t == 6 else PLAN)[k][c]
+
+    def add(q, fn, r, w, busy, lat, sem=None, move=0.0, port=0.0):
         deps = {}
         for k in list(w) + [k for k in r if k[0] == "#"]:
             for j in readers.get(k, []) + ([last[k]] if k in last else []):
@@ -196,8 +282,8 @@ def rank_program(g, core, T, topo):
         for k in w:
             if k[0] == "~" and k in last:
                 deps[last[k]] = False
-        ops.append(dict(q=q, fn=fn, deps=deps, busy=busy, lat=lat, sem=sem, move=move,
-                        gather=sem is None and any(k[:2] in ("la", "lb", "ll") for k in r)))
+        ops.append(dict(due=due[0], q=q, fn=fn, deps=deps, busy=busy, lat=lat, sem=sem, move=move, port=port,
+                        gather=sem is None and any(k[:2] in ("la", "lb", "ll", "ly") for k in r)))
         for k in r:
             readers.setdefault(k, []).append(len(ops) - 1)
         for k in w:
@@ -208,27 +294,29 @@ def rank_program(g, core, T, topo):
         us = max(n, 64) * CYC + FIX[q]
         add(q, lambda s: fn().then_inc(s, 1), r, w, us, us)
 
-    def fill(ap, x, w):
-        op("v", lambda: g.vector.memset(ap, x), [], w)
-
     def newsem(n):
         nd[0] += 1
         return ("d%d" % (nd[0] - 1), n)
 
     def dma(q, out, in_, r, w, us=0.15, **kw):
         add(q, lambda s: Q[q].dma_start(out, in_, **kw).then_inc(s, 16), r, w, 1.0 if q == "g" else 0.06,
-            DMA + us + (1.0 if q == "g" else 0.0), newsem(16), us)
+            DMA + us + (0.5 if q == "g" else 0.0), newsem(16), us)
 
-    def send(j, srcs, stage, t, r):
-        rid, pid = topo.addr(hs[j], core)
-        e = topo.engines(core, hs[j])
-        tr = RemoteDMATransfer(dst_ids=[DstId(rid=rid, pnc=pid)] * 2, dma_engine_mask=mask_of(e),
-                               remote_sem=T.sem["hin%d" % (t + 1)], srcs=srcs, dsts=[stage[t, 0:128, :], stage[t, 128:256, :]],
-                               alu_op=1 if len(srcs) > 1 else 0)
-        add("g", lambda s: g.remote_dma_fused([tr], local_sem=s), r, ["sent%d.%d" % (j, t)], 0.4, DMA + 1.0, newsem(len(e)))
+    def send(k, srcs, t, r):
+        trs, stage = [], staged(T, k, t)
+        for j in ((2,) if k == "c" else (0, 1)):
+            rid, pid = topo.addr(hs[j], core)
+            trs.append(RemoteDMATransfer(dst_ids=[DstId(rid=rid, pnc=pid)] * 2, dma_engine_mask=mask_of(feed(T, topo, rank, j)),
+                                         remote_sem=T.sem["h%s%d" % (k, t)], srcs=srcs, dsts=[stage[0:128, :], stage[128:256, :]],
+                                         alu_op=1 if len(srcs) > 1 else 0))
+        us = 0.7 if k == "c" else 1.3
+        add("g", lambda s: g.remote_dma_fused(trs, local_sem=s), r, ["sent" + k + str(t)], 0.5, DMA + us, newsem(nall), us)
 
-    def arrives(key, s, j, t, us=FAR):
-        add("x", None, ["sent%d.%d" % (j, t)], [key], 0.0, us, (s, nall))
+    def arrives(key, k, t):
+        hand = HANDS[k == "c"]
+        j = hand.index((k, t))
+        add("x", None, ["sent%s%d" % x for x in hand[max(j - 1, 0):j + 1]], [key], 0.0, FAR + 2.0 * (j == 0),
+            ("a%s%d" % (k, t), nall * {"c": 2, "m": 4, "y": 3}[k] // 2), 0.0, 0.9 if k == "c" else 1.8)
 
     def ts(out, in0, s1, s2, o0, o1, r, w, n=K):
         if o1 is None:
@@ -242,21 +330,25 @@ def rank_program(g, core, T, topo):
     def cp(out, a, r, w, n=K):
         op("v", lambda: g.vector.tensor_copy(out, a), r, w, n)
 
+    def scan(out, d0, d1, r, w, n):
+        op("v", lambda: g.vector.tensor_tensor_scan(out, d0, d1, 0.0, OP.mult, OP.add), r, w, n)
+
     def act(out, a, f, r, w, bias=0.0, scale=1.0, n=K):
         op("a", lambda: g.scalar.activation(out, a, f, bias=bias, scale=scale), r, w, n)
 
-    def pe(mms, r, w, n):
+    def pe(mms, r, w):
         def run():
             for a in mms:
                 ins = g.tensor.matmul(*a)
             return ins
-        op("p", run, r, w, n * PEC)
+        op("p", run, r, w, PEC * sum(max(a[2].shape[1], min(64, a[1].shape[1])) for a in mms))
 
     def iota(out, pat, base, cm, w, flt=True):
+        n = 2 * int(np.prod([p[1] for p in pat]))
         if flt:
-            op("g", lambda: g.iota(out, pat, base, cm, allow_small_or_imprecise_dtypes=True), [], w, 256)
+            op("g", lambda: g.iota(out, pat, base, cm, allow_small_or_imprecise_dtypes=True), [], w, n)
         else:
-            op("g", lambda: g.iota(out, pat, base, cm), [], w, 256)
+            op("g", lambda: g.iota(out, pat, base, cm), [], w, n)
 
     def sel(out, a, pat, base, cm, r, w):
         op("g", lambda: g.affine_select(out, a, pat, OP.is_ge, 0.0, base, cm), r, w, 256)
@@ -288,11 +380,14 @@ def rank_program(g, core, T, topo):
     def blk(t, j, n=1, w=K):
         return t[:, j * w:(j + n) * w]
 
-    def ch(t, c):
-        return t[:, c * C:(c + 1) * C]
+    def ch(t, c, o=0):
+        return t[:, o + c * C:o + (c + 1) * C]
 
-    def cx(t, c):
-        return t[:, CH[c][0]:CH[c][1]]
+    def cx(t, c, o=0):
+        return t[:, o + CH[c][0]:o + CH[c][1]]
+
+    def lx(t, j, c):
+        return t[:, j * K + CH[c][0] // 16:j * K + CH[c][1] // 16]
 
     def ks(n):
         return ["%s.%d" % (n, c) for c in range(3)]
@@ -300,342 +395,408 @@ def rank_program(g, core, T, topo):
     def bank(j):
         return T["b%d" % j]
 
-    def compact(bk, j, z, zi, src, o, r):
-        pe([(blk(bank(bk), j), z[:, zi * 144 + 15 - i:zi * 144 + 143 - i], src[:, o + i:o + V:16], i == 0, i == 15)
-            for i in range(16)], r + ["zz"], ["#%d" % bk], V)
+    def mat(j):
+        return blk(T.mb, j, 1, 128)
+
+    def sums(z, zi, src, o, run=False, a=0, b=V):
+        return [(z[:, zi * 144 + 15 - i:zi * 144 + 143 - i], src[:, o + i * K:o + (i + 1) * K] if run else src[:, o + a + i:o + b:16])
+                for i in range(16)]
+
+    def group(out, terms, r, bk):
+        pe([(out, a, b, j == 0, j == len(terms) - 1) for j, (a, b) in enumerate(terms)], r, ["#%d" % bk])
 
     m = [T.m0, T.m1, T.m2]
     yy = [T.yy0, T.yy1, T.yy2]
-    cc = [T.cc0, T.cc1, T.cc2]
     hh = [T.hh0, T.hh1, T.hh2]
     sp = [T.sp0, T.sp1]
-    ver = [T.ver0, T.ver1, T.ver2]
-    oh = [T.oh0, T.oh1]
-    rb = [T.rb0, T.rb1]
-    col = T.col
-    vv, vl, pv, wid, l1 = [blk(T.b5, j) for j in range(5)]
-    sw = T.cc0
+    xv = [T.xv0, T.xv1, T.xv2]
+    oh, oo = [T.aq, T.oh1], [SO, 0]
+    col, sw = T.col, T.aq
+    ID, W4, O4, NEG, LE, LW, P15, M15, X16, P60, M60 = range(11)
+    o4 = T.fw
 
-    def zb(t):
-        return 2 if t % 2 else 7
+    def sign(j, c):
+        return cx(hh[j], c) if c else blk(T.sg, j, 1, NB)
+
+    def signs(j):
+        return ["g%d" % j] + ks("h%d" % j)[1:]
+
+    def slot(t, j):
+        return T.dk[:, (t - 2) * DK + j:(t - 2) * DK + 4 * K:4]
+
+    def held(t):
+        return T.dk[:, (t - 2) * DK + 4 * K + 1:(t - 1) * DK:2]
 
     dma("s", T.curb[:], T.cur[:], [], ["cur", "~s"])
     dma("a", T.dh[0, 128:256, :], T.s0[:, 0:NB], [], ["dh1", "~a"])
     dma("s", T.dh[0, 0:128, :], T.s0[:, 0:NB], [], ["dh0", "~s"])
-    dma("a", ch(T.ptb, 0), ch(T.pt, 0), [], ["pt.0", "~a"], 0.65)
-    dma("s", ch(T.ptb, 1), ch(T.pt, 1), [], ["pt.1", "~s"], 0.65)
-    dma("a", ch(T.ptb, 2), ch(T.pt, 2), [], ["pt.2", "~a"], 0.65)
-    dma("s", sw[:, 0:V], T.s0[:], [], ["c0", "~s"], 1.0)
+    dma("a", ch(T.ptb, 0), ch(T.pt, 0), [], ["pt.0", "~a"], 0.55)
+    dma("s", sw[:, 0:V], T.s0[:], [], ["sw", "~s"], 0.9)
+    dma("a", ch(T.ptb, 1), ch(T.pt, 1), [], ["pt.1", "~a"], 0.65)
 
-    iota(T.pc[:, 0:2], [[0, 2]], 0, 1, ["pc"], False)
+    at(0.1)
+    iota(T.pc[:, 0:1], [[0, 1]], 0, 1, ["pc"], False)
     iota(T.gi[:], [[1, 8], [0, 16]], 0, -1, ["gi"])
     iota(T.ci[:], [[1, 144]], 0, -1, ["ci"])
     iota(T.lw[:], [[0, 8], [-2, 16]], 0, 0, ["lw"])
-    fill(T.one[:], 1.0, ["one"])
-    for c in range(3):
-        fill(T.vs[:, 3 * K + CH[c][0] // 16:3 * K + CH[c][1] // 16], float(WD[c]), ["vs3"])
-    ts(T.pc[:, 2:3], T.pc[:, 0:1], 15, None, OP.bitwise_and, None, ["pc"], ["pc2"])
-    ts(blk(T.mb, 4, 1, 128), T.gi[:], 0.0, None, OP.is_equal, None, ["gi"], ["le"])
-    cp(col[:, 0:1], T.pc[:, 2:3], ["pc2"], ["i"])
-    ts(T.pc[:, 3:4], T.pc[:, 0:1], 3, None, OP.bitwise_and, None, ["pc"], ["pc3"])
-    ts(col[:, 1:2], col[:, 0:1], -1.0, 15.0, OP.mult, OP.add, ["i"], ["c15"])
-    ts(col[:, 2:3], col[:, 0:1], col[:, 0:1], -1.0, OP.mult, OP.mult, ["i"], ["isq"])
-    ts(col[:, 4:5], col[:, 0:1], 1.5, None, OP.is_le, None, ["i"], ["wa"])
-    ts(col[:, 9:10], col[:, 0:1], float(K), None, OP.mult, None, ["i"], ["i96"])
+    iota(T.pc[:, 1:2], [[0, 1]], 1, 1, ["pc1"], False)
+    op("v", lambda: g.vector.memset(T.one[:], 1.0), [], ["one"])
+    op("v", lambda: g.vector.memset(T.kh[:], 1024.0), [], ["k1024"], 64)
+    ts(T.pc[:, 2:3], T.pc[:, 0:1], 15, None, OP.bitwise_and, None, ["pc"], ["pc2"], 64)
+    ts(mat(LE), T.gi[:], 0.0, None, OP.is_equal, None, ["gi"], ["le"], 128)
+    cp(col[:, 0:1], T.pc[:, 2:3], ["pc2"], ["i"], 64)
+    ts(T.pc[:, 4:6], T.pc[:, 0:2], 3, None, OP.bitwise_and, None, ["pc", "pc1"], ["pc3"], 64)
+    ts(col[:, 1:2], col[:, 0:1], -1.0, 15.0, OP.mult, OP.add, ["i"], ["c15"], 64)
+    ts(col[:, 2:3], col[:, 0:1], col[:, 0:1], -1.0, OP.mult, OP.mult, ["i"], ["isq"], 64)
+    ts(col[:, 3:4], col[:, 2:3], 1.0, None, OP.add, None, ["isq"], ["bias"], 64)
+    ts(mat(ID), T.ci[:, 0:128], 0.0, None, OP.is_equal, None, ["ci"], ["id"], 64)
+    ts(T.gi[:], T.gi[:], -8.0, None, OP.is_equal, None, ["gi", "le"], ["gi"], 128)
+    tt(T.lw[:], T.gi[:], T.lw[:], OP.mult, ["gi", "lw"], ["lw"], 256)
+    tt(mat(LW), mat(LE), T.lw[:], OP.add, ["le", "lw"], ["lwm"], 256)
+    ts(blk(T.zh, 0, 1, 144), T.ci[:], col[:, 1:2], None, OP.is_equal, None, ["ci", "c15"], ["z1"], 72)
+    ts(T.ih[:], T.ci[:, 0:128], 0.0, None, OP.is_equal, None, ["ci"], ["ih"], 64)
+    at(1.5)
+    act(T.kb[:, 7 * K:7 * K + 1], col[:, 0:1], AF.Sigmoid, ["i"], ["wa"], bias=384.0, scale=-256.0, n=1600)
     for j in range(4):
-        ts(col[:, 5 + j:6 + j], T.pc[:, 3:4], float(j), None, OP.is_equal, None, ["pc3"], ["wq"])
-    ts(col[:, 3:4], col[:, 2:3], 1.0, None, OP.add, None, ["isq"], ["bias"])
-    ts(blk(T.mb, 0, 1, 128), T.ci[:, 0:128], 0.0, None, OP.is_equal, None, ["ci"], ["id"])
-    tt(blk(T.mb, 5, 1, 128), blk(T.mb, 4, 1, 128), T.lw[:], OP.mult, ["le", "lw"], ["lwm"])
-    ts(blk(T.zh, 0, 1, 144), T.ci[:], col[:, 1:2], None, OP.is_equal, None, ["ci", "c15"], ["zz"])
-    ts(blk(T.zb, 0, 1, 144), T.ci[:], col[:, 1:2], 0.5, OP.is_equal, OP.mult, ["ci", "c15"], ["zz"])
-    ts(blk(T.zb, 1, 1, 144), T.ci[:], col[:, 1:2], col[:, 4:5], OP.is_equal, OP.mult, ["ci", "c15", "wa"], ["zz"])
-    ts(blk(T.zb, 2, 1, 144), T.ci[:], col[:, 1:2], col[:, 0:1], OP.is_equal, OP.mult, ["ci", "c15", "i"], ["zz"])
+        ts(col[:, 5 + j:6 + j], T.pc[:, 4:5], float(j), None, OP.is_equal, None, ["pc3"], ["wq%d" % j], 64)
+    cp(col[:, 9:10], T.pc[:, 5:6], ["pc3"], ["wr"], 64)
+    act(col[:, 10:11], col[:, 0:1], AF.Identity, ["i"], ["w5"], bias=5.0, n=64)
+    for j, x, k in ((NEG, -1.0, "neg"), (P15, float(V), "p15"), (M15, -float(V), "m15"), (X16, 16.0, "x16"),
+                    (P60, 4.0 * V, "p60"), (M60, -4.0 * V, "m60")):
+        act(mat(j), mat(ID), AF.Identity, ["id"], [k], scale=x, n=128)
     sel(T.bd1[:], T.one[:], [[16, 8], [0, 16]], 15, -1, ["one"], ["bd1"])
     iota(T.t4[:, 256:384], [[1, 128]], 255, -1, ["t4w"], False)
+    at(2.4)
     add("g", lambda s: spread(g, core, T, topo, rank, T.dh[0], sw, T.sem.as1, s), ["dh0", "dh1"], ["sent0.0"], 2.0, FAR + 1.5, newsem(nall))
-    arrives("c0.bus", "as1", 0, 0, 0.3)
+    add("x", None, ["sent0.0"], ["sw.bus"], 0.0, 0.3, ("as1", nall))
 
-    ts(blk(T.ci2, 0), T.curb[:], 15, None, OP.bitwise_and, None, ["cur"], ["cs"])
-    ts(blk(T.ci2, 1), T.curb[:], 4, None, OP.arith_shift_right, None, ["cur"], ["ct"])
-    cp(blk(T.ft, 2, 2), T.ci2[:], ["cs", "ct"], ["f1"])
-    tt(blk(T.ft, 0, 2), T.ci2[:], T.ci2[:], OP.mult, ["cs", "ct"], ["f0"])
-    for f, q in ((2, "s"), (0, "a"), (3, "s"), (1, "a")):
-        dma(q, T.aq[0:8, f * V:(f + 1) * V], blk(T.ft, f), ["f%d" % (f // 2)], ["fw%d" % f, "aq%d" % f])
-    for j in range(4):
-        ts(blk(T.zh, 1 + j, 1, 144), T.ci[:], col[:, 1:2], col[:, 5 + j:6 + j], OP.is_equal, OP.mult, ["ci", "c15", "wq"], ["zz"])
+    for tb, (o, x) in enumerate(((OP.bitwise_and, 15), (OP.arith_shift_right, 4))):
+        at(1.0 + 0.1 * tb)
+        ts(blk(T.ci2, tb), T.curb[:], x, None, o, None, ["cur"], ["ci%d" % tb])
+        cp(blk(T.ft, 2 + tb), blk(T.ci2, tb), ["ci%d" % tb], ["f%d" % (2 + tb)])
+        act(blk(T.ft, tb), blk(T.ft, 2 + tb), AF.Square, ["f%d" % (2 + tb)], ["f%d" % tb])
+        for f, q in ((2 + tb, "s"), (tb, "a")):
+            dma(q, T.fw[f // 2 * 8:f // 2 * 8 + 8, tb * V:(tb + 1) * V], blk(T.ft, f), ["f%d" % f], ["fw%d" % f], 0.25)
+        if tb == 0:
+            dma("s", ch(T.ptb, 2), ch(T.pt, 2), ["f0"], ["pt.2"], 0.65)
+
+    z0, zhalf = blk(T.zh, 0, 1, 144), blk(T.zb, 0, 1, 144)
+    at(8.5)
+    tt(col[:, 11:14], col[:, 6:9], col[:, 5:8], OP.subtract, ["wq%d" % j for j in range(4)], ["wd"], 64)
+    for j in range(7):
+        c = 5 + j if j < 4 else 7 + j
+        ts(blk(T.zh, 1 + j, 1, 144), z0, col[:, c:c + 1], None, OP.mult, None, ["z1", "wq%d" % j if j < 4 else "wd"], ["zh%d" % (1 + j)], 72)
+    ts(blk(T.zh, 8, 1, 144), z0, -1.0, None, OP.mult, None, ["z1"], ["zh8"], 72)
+    ts(zhalf, z0, 0.5, None, OP.mult, None, ["z1"], ["zb0"], 72)
+    ts(col[:, 14:16], col[:, 9:11], 2.0, None, OP.mult, None, ["wr", "w5"], ["w2"], 64)
+    ts(blk(T.zb, 1, 1, 144), z0, T.kb[:, 7 * K:7 * K + 1], None, OP.mult, None, ["z1", "wa"], ["zb1"], 72)
+    at(14.0)
+    act(blk(T.zb, 2, 1, 144), zhalf, AF.Identity, ["zb0", "w2"], ["zb2"], scale=col[:, 14:15], n=144)
+    act(blk(T.zb, 3, 1, 144), zhalf, AF.Identity, ["zb0", "w2"], ["zb3"], scale=col[:, 15:16], n=144)
+    at(4.5)
     sel(T.bd[:], T.bd1[:], [[-16, 8], [0, 16]], 0, 1, ["bd1"], ["bd"])
     iota(T.t4[:, 0:128], [[0, 8], [1, 4], [0, 4]], 255, -1, ["t4a"], False)
-    iota(T.t4[:, 128:256], [[0, 8], [1, 4], [1, 4]], 256, -1, ["t4a"], False)
-    iota(blk(T.vs, 0), [[16, K]], 0, 0, ["vs"])
+    iota(T.t4[:, 128:256], [[0, 8], [1, 4], [1, 4]], 256, -1, ["t4b"], False)
+    at(8.0)
+    iota(blk(T.vs, 0), [[16, K]], 0, 0, ["vs0"])
+    at(15.5)
     for c in range(3):
-        iota(T.vs[:, K + CH[c][0] // 16:K + CH[c][1] // 16], [[16, (CH[c][1] - CH[c][0]) // 16]], 0, 0, ["vs"])
-    iota(blk(T.vs, 2), [[1, K]], 0, 0, ["vs"])
+        n = WD[c] // 16
+        iota(lx(T.vs, 1, c), [[16, n]], 0, 0, ["vs1.%d" % c])
+        iota(lx(T.vs, 2, c), [[-16, n]], WD[c], 0, ["vs2.%d" % c])
+        iota(lx(T.vs, 3, c), [[0, n]], WD[c], 0, ["vs3.%d" % c])
+    at(8.5)
+    iota(blk(T.kb, 0), [[16, K]], 0, 0, ["vhi"])
+    iota(T.th[:], [[64, 9], [0, 64]], V, 0, ["th"])
+    iota(T.aq[:, AY + V:AY + W], [[0, 9], [1, 64]], 0, 0, ["ty"])
+    at(11.0)
+    dma("s", T.aq[0:128:16, AY + V:AY + W], T.th[0:128:16, :], ["th", "ty"], ["ty"], 0.25)
+    for t in range(2, 7):
+        at(7.5 if t == 2 else START[t - 1] + 7.5)
+        if t < 6:
+            iota(T.dk[:, (t - 2) * DK:(t - 2) * DK + 4 * K], [[0, K], [1, 4]], 0, 0, ["k1%d" % t, "n3%d" % t])
+        iota(T.dk[:, (t - 2) * DK + 4 * K:(t - 1) * DK], [[0, K], [1, 2]], 0, 0, ["kh%d" % t])
+    for t in range(2, 6):
+        at(START[t - 1] + 3.5)
+        iota(blk(T.kb, t + 1), [[0, K]], (t - 2) * V + (SO if t % 2 == 0 else SO - AY), 0, ["ck%d" % t])
+    at(20.0)
+    iota(T.dt[:], [[0, 5 * K]], 0, 0, ["dt"])
 
     def onehot(tb):
         for c in range(3):
-            pe([(bank(c)[:], T.mb[0:8, 512:640], T.aq[0:8, tb * V + c * C:tb * V + (c + 1) * C], True, False),
-                (bank(c)[:], T.mb[0:8, 640:768], T.aq[0:8, (2 + tb) * V + c * C:(2 + tb) * V + (c + 1) * C], False, True)],
-               ["le", "lwm", "fw%d" % tb, "fw%d" % (2 + tb), "aq%d" % tb, "aq%d" % (2 + tb)], ["#%d" % c], 2 * C)
-            act(ch(oh[tb], c), bank(c)[:], AF.Relu, ["#%d" % c, "bias"], ["oh%d.%d" % (tb, c)], bias=col[:, 3:4], scale=-1.0, n=C)
+            pe([(bank(c)[:], T.mb[0:16, LW * 128:(LW + 1) * 128], T.fw[0:16, tb * V + c * C:tb * V + (c + 1) * C], True, True)],
+               ["lwm", "fw%d" % tb, "fw%d" % (2 + tb)], ["#%d" % c])
+            act(ch(oh[tb], c, oo[tb]), bank(c)[:], AF.Relu, ["#%d" % c, "bias"], ["oh%d.%d" % (tb, c)], bias=col[:, 3:4], scale=-1.0, n=C)
 
-    def masked(out, on, tab, tn, mat, mn, tb):
+    def masked(out, on, tab, tn, mt, mn, tb):
         for c in range(3):
             bk = 3 + c % 2
-            pe([(bank(bk)[:], blk(T.mb, mat, 1, 128), ch(oh[tb], c), True, True)], [mn, "oh%d.%d" % (tb, c)], ["#%d" % bk], C)
+            pe([(bank(bk)[:], mat(mt), ch(oh[tb], c, oo[tb]), True, True)], [mn, "oh%d.%d" % (tb, c)], ["#%d" % bk])
             tt(ch(out, c), ch(tab, c), bank(bk)[:], OP.mult, ["#%d" % bk, "%s.%d" % (tn, c)], ["%s.%d" % (on, c)], C)
-
-    def rows(k0, n):
-        act(blk(T.qh, k0, n), blk(T.qs, k0, n), AF.Identity, ["qs%d" % k0], ["qh%d" % k0], n=n * K)
-        tt(blk(T.ql, k0, n), blk(T.qs, k0, n), blk(T.qh, k0, n), OP.subtract, ["qs%d" % k0, "qh%d" % k0], ["ql%d" % k0], 2 * n * K)
-        for k in range(k0, k0 + n):
-            dma("s", T.aq[0:128:16, (4 + k) * V:(5 + k) * V], blk(T.qh, k), ["qh%d" % k0, "aq%d" % (4 + k)], ["aqh%d" % k])
-            dma("s", T.aq[1:128:16, (4 + k) * V:(5 + k) * V], blk(T.ql, k), ["ql%d" % k0, "aq%d" % (4 + k)], ["aql%d" % k])
 
     def la(t, c):
         j = 0 if t < 3 else t - 1
-        return T.la[:, j * K + CH[c][0] // 16:j * K + CH[c][1] // 16], "la%d" % (j + 1)
+        return lx(T.la, j, c), "la%d.%d" % (j + 1, c > 0)
+
+    def listed(t, h, terms, r):
+        a, b = HALF[h][0] // 16, HALF[h][1] // 16
+        group(T.b6[:, 4 * a:4 * b:4], terms, r, 6)
+        cp(T.la[:, (t - 1) * K + a:(t - 1) * K + b], T.b6[:, 4 * a:4 * b:4], ["#6"], ["la%d.%d" % (t, h)], b - a)
 
     def product(t):
         mt, n, u = m[t % 3], "m%d" % (t % 3), (t + 1) % 3
         e = 1.0 if t % 2 else -1.0
+        mv, vn = T.mv, ks("mv")
+        at(t, "g1")
         if t > 1:
-            arrives(n + ".bus", "am%d" % t, 0, t - 1)
-        if t < 6:
-            dma("s", cc[u][:, 0:V], hh[t % 3][:], ks("h%d" % (t % 3)), ["c%d" % u], 1.0)
+            arrives(n + ".bus", "m", t)
+            vn[0] = n + ".bus"
+        else:
+            mt, n, mv, vn = hh[0], "h0", T.zp, ks("zp")
         for c in range(3):
             o, on = la(t, c)
-            tt(cx(T.pp, c), mt[:, 0:W].indirect(o), cx(T.mv, c), OP.mult, ks(n) + [n + ".bus", on, "mv.%d" % c], ["p.%d" % c], GA * WD[c])
+            at(t, "g1", c)
+            tt(cx(T.pp, c), mt[:, 0:W].indirect(o), cx(mv, c), OP.mult, ks(n) + [n + ".bus", on, vn[c]], ["p.%d" % c], GA * WD[c])
         for c in range(3):
             if t < 6:
-                act(cx(m[u], c), cx(T.pp, c), AF.Abs, ["p.%d" % c] + ["y1.bus"] * (t == 1), ["m%d.%d" % (u, c)], bias=1.0, scale=-2.0, n=WD[c])
-                dma("s", cx(T.mv, c), cx(m[u], c), ["m%d.%d" % (u, c)], ["mv.%d" % c], WD[c] / 780)
-            if c == 0 and t < 6:
-                send(0, [cx(m[u], 0)], T.df, t, ["m%d.0" % u])
-            if c in SV.get(t, ()):
+                at(t, "e2", c)
+                act(cx(m[u], c), cx(T.pp, c), AF.Abs, ["p.%d" % c], ["m%d.%d" % (u, c)], bias=1.0, scale=-2.0, n=WD[c])
+                if c == 0:
+                    send("m", [cx(m[u], 0)], t + 1, ["m%d.0" % u])
+                else:
+                    dma("s", cx(T.mv, c), cx(m[u], c), ["m%d.%d" % (u, c)], ["mv.%d" % c], 0.75)
+                at(t, "e3", c)
+                act(sign(u, c), cx(T.pp, c), AF.Sign, ["p.%d" % c], [signs(u)[c]], bias=e * (1.875 + 2.0 ** -23), scale=-3.75 * e, n=WD[c])
+                if c == 0:
+                    send("c", [sign(t % 3, 0), sign(u, 0)], t + 1, ["g%d" % (t % 3), "g%d" % u])
+            at(t, "e1", c)
+            if c in EV.get(t, ()):
                 ts(cx(sp[t % 2], c), cx(T.pp, c), -2.0, 1.0, OP.mult, OP.add, ["p.%d" % c], ["sp%d.%d" % (t % 2, c)], WD[c])
             else:
                 act(cx(sp[t % 2], c), cx(T.pp, c), AF.Identity, ["p.%d" % c], ["sp%d.%d" % (t % 2, c)], bias=1.0, scale=-2.0, n=WD[c])
-            if t == 6:
-                continue
-            act(cx(hh[u], c), cx(sp[t % 2], c), AF.Sign, ["sp%d.%d" % (t % 2, c)], ["h%d.%d" % (u, c)], bias=e * EPS, scale=e, n=WD[c])
-            if c == 0:
-                send(1, [cx(hh[t % 3], 0), cx(hh[u], 0)], T.dh, t, ["h%d.0" % (t % 3), "h%d.0" % u])
         if t < 6:
-            dma("g", cc[u][:, 0:V], hh[u][:], ks("h%d" % u) + ["c%d" % u], ["c%d" % u], 2.0, accum_op=OP.add)
+            at(t, "add")
+            dma("g", hh[t % 3][:, NB:V], hh[u][:, NB:V], ks("h%d" % u)[1:] + ks("h%d" % (t % 3))[1:], ks("h%d" % (t % 3))[1:], 1.2,
+                accum_op=OP.add)
 
     def drive(t):
-        yt, n = yy[t % 3], "y%d" % (t % 3)
-        if t > 1:
-            arrives(n + ".bus", "ay%d" % t, 2, t - 1)
+        yt, n, u = yy[t % 3], "y%d" % (t % 3), (t + 1) % 3
+        at(t, "g3")
+        arrives(n + ".bus", "y", t)
         for c in range(3):
             o, on = la(t, c)
-            tt(cx(T.xx, c), yt[:, 0:W].indirect(o), cx(sp[t % 2], c), OP.mult,
-               ks(n) + [n + ".bus", on, "sp%d.%d" % (t % 2, c)], ["x.%d" % c], GA * WD[c])
-            act(blk(ver[c], 6 - t, 1, WD[c]), cx(T.xx, c), AF.Tanh, ["x.%d" % c], ["v%d.%d" % (t, c)], n=WD[c])
-
-    def blend(t, c, q="a"):
-        u, w = (t + 1) % 3, CH[c][1] - CH[c][0]
-        vs = ["v%d.%d" % (j, c) for j in range(1, t + 1)] + ["lb%d" % (t + 1)]
-        j = (2 * t - 1) * K
-        src = blk(ver[c], 5, 1, w) if t == 1 else ver[c][:, (6 - t) * w:6 * w].indirect(T.lb[:, j + CH[c][0] // 16:j + CH[c][1] // 16])
-        if t < 6:
-            act(cx(yy[u], c), src, AF.Identity, vs, ["y%d.%d" % (u, c)], bias=1.0, n=w * (GA if t > 1 else 1))
-            if c == 0:
-                send(2, [cx(yy[u], 0)], T.df, t, ["y%d.0" % u])
-        else:
-            if q == "a":
-                act(cx(T.pp, c), src, AF.Identity, vs, ["p.%d" % c], n=w * GA)
+            w = WD[c]
+            at(t, "g3", c)
+            tt(blk(xv[c], 6 - t, 1, w), yt[:, 0:W].indirect(o), cx(sp[t % 2], c), OP.mult,
+               ks(n) + [n + ".bus", on, "sp%d.%d" % (t % 2, c)], ["x%d.%d" % (t, c)], GA * w)
+            at(t, "e4", c)
+            vs = ["x%d.%d" % (j, c) for j in range(1, t + 1)] + ["ly%d" % t] * (t > 1)
+            src = blk(xv[c], 5, 1, w) if t == 1 else xv[c][:, (6 - t) * w:6 * w].indirect(lx(T.ly, t - 2, c))
+            if t < 6:
+                act(cx(yy[u], c), src, AF.Sigmoid, vs, ["y%d.%d" % (u, c)], scale=4.0, n=w * GA if t > 1 else w)
+                if c == 0:
+                    send("y", [cx(yy[u], 0)], t + 1, ["y%d.0" % u])
             else:
-                cp(cx(T.pp, c), src, vs, ["p.%d" % c], w * GA)
-            dma("s", cx(T.y, c), cx(T.pp, c), ["p.%d" % c], [], w / 780)
+                act(cx(m[1], c), src, AF.Sigmoid, vs, ["m1.%d" % c], scale=4.0, n=w * GA)
+                ts(cx(m[1], c), cx(m[1], c), 2.0, -1.0, OP.mult, OP.add, ["m1.%d" % c], ["m1.%d" % c], w)
+                dma("s", cx(T.y, c), cx(m[1], c), ["m1.%d" % c], [], w / 1100)
 
     def trigger(t):
-        n = "c%d" % (t % 3)
-        arrives(n + ".bus", "ac%d" % t, 1, t - 1)
-        for c in range(2):
-            a, b = c * V // 2, (c + 1) * V // 2
-            tt(T.zp[:, a:b], cc[t % 3][:, 0:W].indirect(T.lb[:, (2 * t - 4) * K + a // 16:(2 * t - 4) * K + b // 16]),
-               hh[t % 3][:, a:b], OP.mult, [n, n + ".bus", "lb%d" % t] + ks("h%d" % (t % 3)), ["zp"], GA * V / 2)
-        compact(zb(t), 0, T.zb, 0, T.zp, 0, ["zp"])
-
-    def fold():
+        w, n = hh[(t - 1) % 3], "h%d" % ((t - 1) % 3)
+        at(t, "g2")
+        arrives(n + ".bus", "c", t)
         for c in range(3):
-            bk = 3 + c % 2
-            pe([(bank(bk)[:], T.mh[:], ch(rb[1], c), True, True)], ["fk", "rb1.%d" % c], ["#%d" % bk], C)
-            tt(ch(T.ra, c), ch(T.aq, c), bank(bk)[:], OP.mult, ["#%d" % bk, "o4.%d" % c], ["ra.%d" % c], C)
-        for j in range(4):
-            compact(1, j, T.zh, 1 + j, T.ra, 0, ks("ra"))
-        act(blk(T.qt, 1, 4), blk(bank(1), 0, 4), AF.Identity, ["#1"], ["qt1"], bias=1024.0, n=4 * K)
+            at(t, "g2", c)
+            tt(cx(T.zp, c), w[:, 0:W].indirect(lx(T.lb, t - 2, c)), sign(t % 3, c), OP.mult,
+               ks(n) + [n + ".bus", "lb%d" % t, signs(t % 3)[c]], ["zp.%d" % c], GA * WD[c])
+        z = blk(T.b1, 0)
+        group(z, sums(T.zb, 0, T.zp, 0), ks("zp") + ["zb0"], 1)
+        at(t, "k")
+        if t < 6:
+            ts(slot(t, 2), z, 0.5, None, OP.is_ge, None, ["#1"], ["k1%d" % t])
+        ts(slot(t, 3), z, 2.5, None, OP.is_le, None, ["#1"], ["n3%d" % t])
+        at(t, "k", 1)
+        ts(held(t), z, -1.5, None, OP.is_le, None, ["#1"], ["kh%d" % t])
 
     def ahead(t):
-        if t == 2:
-            cp(blk(T.ti, 1), T.c1[:], ["cur1"], ["ri"])
-        else:
-            tt(blk(T.ti, 1), T.c1[:], blk(T.jj, 0), OP.add, ["cur1", "j"], ["ri"], 2 * K)
-        ts(T.rr[:], blk(T.ti, 1), 3, None, OP.bitwise_and, None, ["ri"], ["rr"])
-        ts(T.nx[:], T.rr[:], float(V), float(V * (t - 1)), OP.mult, OP.add, ["rr"], ["nx"])
-        tt(T.nx2[:], T.nx[:], pv, OP.add, ["nx", "vv"], ["nx2"])
-
-    def masks(t):
-        b, k = bank(zb(t)), "#%d" % zb(t)
-        if t < 6:
-            tt(blk(b, 1), blk(b, 0), T.thr[:], OP.is_gt, [k, "thr"], ["k1%d" % t])
-        ts(blk(b, 2), blk(b, 0), 2.5, None, OP.is_ge, None, [k], ["k3%d" % t])
-        ts(blk(b, 3), blk(b, 0), -1.5, None, OP.is_le, None, [k], ["kh%d" % t])
-
-    def held(t):
-        tt(T.be[:], blk(bank(zb(t)), 3), blk(T.vs, 3) if t == 2 else T.bp[:], OP.mult,
-           ["#%d" % zb(t), "kh%d" % t, "vs3", "bp"], ["be"])
+        turns = [slot(j, 3) for j in range(2, t)]
+        r = ["id", "neg", "p15", "m15", "r0", "ck%d" % t, "vhi", "vlo"] + ["n3%d" % j for j in range(2, t)]
+        r0, wrap = blk(T.kb, 8), [blk(T.kb, 2)] * (t > 2)
+        if t > 2:
+            group(blk(T.b2, 2), [(mat(ID), r0)] + [(mat(NEG), x) for x in turns], r, 2)
+            act(wrap[0], blk(T.b2, 2), AF.Sigmoid, ["#2"], ["wrap"], bias=256.0 * (t - 5.5), scale=256.0)
+            r = r + ["wrap", "p60", "m60"]
+        group(T.b6[:, 2:4 * K:4], [(mat(NEG), blk(T.kb, t + 1)), (mat(M15), r0)] + [(mat(P15), x) for x in turns]
+              + [(mat(P60), x) for x in wrap], r, 6)
+        group(T.b6[:, 3:4 * K:4], [(mat(ID), blk(T.kb, j)) for j in (t + 1, 0, 1)] + [(mat(P15), r0)]
+              + [(mat(M15), x) for x in turns] + [(mat(M60), x) for x in wrap], r, 6)
 
     def elect(t):
-        b, k, k1, k3, kh = bank(zb(t)), "#%d" % zb(t), "k1%d" % t, "k3%d" % t, "kh%d" % t
-        pb = blk(b, 4)
-        tt(T.pr[:], blk(b, 1, 2), T.dd[:], OP.mult, [k, k1, k3, "d1", "d3"], ["pr"], 2 * K)
-        held(t)
-        tt(l1, blk(T.pr, 0), pv if t == 2 else vv, OP.add, ["pr", "vv"], ["l1"])
-        tt(pb, blk(b, 3), blk(T.dt, 0) if t == 2 else T.db[:], OP.mult, [k, kh, "db", "dt0"], ["pb"])
-        tt(T.l2[:], l1, blk(T.pr, 1), OP.add, ["l1", "pr"], ["l2"])
-        tt(blk(T.bs, 1), T.be[:], vl, OP.add, ["be", "vv"], ["yl"])
-        cp(T.ll[:], T.l2[:], ["l2"], ["ll"])
-        a0 = 6 - t
-        act(blk(T.aq, a0 - 1, 1, V), T.aq[:, a0 * V:9 * V].indirect(T.ll[:]), AF.Identity,
-            ["ll"] + ["aq%d" % j for j in range(a0, 9)] + ["aq%s%d" % (x, j) for x in "hl" for j in range(5)],
-            ["aq%d" % (a0 - 1)], n=GA * V)
-        compact(6, 0, T.zb, 1, T.aq, (a0 - 1) * V, ["aq%d" % (a0 - 1)])
-        tt(blk(T.bs, 0), pb, blk(T.qt, 0) if t == 2 else blk(T.bs, 0), OP.add, [k, "pb", "b", "qt0"], ["b"])
+        even = t % 2 == 0
+        at(t, "el")
+        scan(T.so[:], T.dk[:, (t - 2) * DK:(t - 2) * DK + 4 * K], T.b6[:, 0:4 * K], ["#6", "k1%d" % t, "n3%d" % t, "nv"], ["so"], 4 * K)
+        ts(T.ll[:], T.so[:, 3:4 * K:4], 0.0 if even else float(AY - SO), None, OP.add, None, ["so"], ["ll"])
+        win = T.aq[:, 0:AY] if even else T.aq[:, SO:AY + W]
+        o = AY if even else 0
+        tabs = ["aq%s%d" % (x, j) for x in "hl" for j in range(1, 5)]
+        old, new = ("ax", "ay") if even else ("ay", "ax")
+        for h, (a, b) in enumerate(HALF):
+            at(t, "el", 1 + h)
+            act(T.aq[:, o + a:o + b], win.indirect(T.ll[:, a // 16:b // 16]), AF.Identity,
+                ["ll", old + "0", old + "1"] + tabs + (["tx", "aqh0", "aql0"] if even else ["ty"]), [new + str(h)], n=GA * (b - a))
+            listed(t + 1, h, sums(T.zb, 1, T.aq, o, False, a, b), [new + str(h), "zb1"])
+        if t < 5:
+            at(t, "el", 3)
+            ahead(t + 1)
+
+    def keep(t):
+        at(t, "keep")
+        scan(T.yo[:], T.dk[:, (t - 2) * DK + 4 * K:(t - 1) * DK], T.b5[:, 0:2 * K], ["kh%d" % t, "bp", "vl"], ["yo"], 2 * K)
+        cp(blk(T.ly, t - 2), T.yo[:, 1:2 * K:2], ["yo"], ["ly%d" % t])
+        if t < 6:
+            tt(T.b5[:, 0:2 * K:2], T.yo[:, 1:2 * K:2], blk(T.b5, 2), OP.add, ["yo", "wv"], ["bp"])
+
+    def turn(t):
+        at(t, "turn")
         if t == 2:
-            cp(T.jj[:], blk(b, 2, 2), [k, k3, kh], ["j"], 2 * K)
-        else:
-            tt(T.jj[:], T.jj[:], blk(b, 2, 2), OP.add, [k, k3, kh, "j"], ["j"], 2 * K)
-        cp(blk(T.lb, 2 * t - 2, 2), T.bs[:], ["b", "yl"], ["lb%d" % (t + 1)], 2 * K)
-
-    def prepare(t):
-        a, n = blk(bank(6), 0), t - 2
-        tt(T.bp[:], T.be[:], wid, OP.add, ["be", "vv"], ["bp"])
-        if t == 6:
+            at(t, "turn", 1)
+            tt(blk(T.to, 0), T.b7[:, 3:5 * K:5], held(t), OP.mult, ["#7", "kh2"], ["to0"])
+            tt(blk(T.to, 1), T.b7[:, 4:5 * K:5], blk(T.to, 0), OP.add, ["#7", "to0"], ["to"])
+            ts(blk(T.lb, 1), blk(T.to, 1), 1024.0, None, OP.add, None, ["to"], ["lb3"])
+            at(START[3] + 1.0)
+            for k in range(1, 4):
+                group(T.b7[:, 3 - k:5 * K:5], sums(T.zh, 4 + k, T.ra, 0), ks("ra") + ["zh%d" % (4 + k)], 7)
             return
-        ahead(t)
-        for k in range(n):
-            ts(blk(T.b4, k), blk(T.jj, 1), k + 0.5, None, OP.is_ge, None, ["j"], ["#4"])
-        tt(blk(T.b3, 0, n), blk(T.b4, 0, n), blk(T.f2, 0, n), OP.mult, ["#4", "f2"], ["#3"], n * K)
-        ts(T.thr[:], a, V - 0.5, 2.0, OP.is_ge, OP.mult, ["#6"], ["thr"])
-        tt(blk(T.dd, 0), a, blk(T.vs, 0), OP.subtract, ["#6", "vv"], ["d1"])
-        acc, an = blk(T.dt, 0), "dt0"
-        for k in range(n):
-            out, on = (T.db[:], "db") if k == n - 1 else (blk(T.ga, k), "ga%d" % k)
-            tt(out, acc, blk(T.b3, k), OP.add, [an, "#3"], [on])
-            acc, an = out, on
-            if k == 0:
-                tt(blk(T.dd, 1), T.nx2[:], a, OP.subtract, ["#6", "nx2"], ["d3"])
+        group(blk(T.b3, 0), [(mat(ID), held(j)) for j in range(2, t + 1)], ["id"] + ["kh%d" % j for j in range(2, t + 1)], 3)
+        for k in range(1, t):
+            act(T.dt[:, 5 - k:5 * K:5], blk(T.b3, 0), AF.Sigmoid, ["#3", "dt"], ["dt%d" % k], bias=128.0 - 256.0 * k, scale=256.0)
+        at(t, "turn", 1)
+        scan(T.to[:], T.dt[:], T.b7[:, 0:5 * K], ["#7", "dt"] + ["dt%d" % k for k in range(1, t)], ["to"], 5 * K)
+        ts(blk(T.lb, t - 1), T.to[:, 4:5 * K:5], 1024.0, None, OP.add, None, ["to"], ["lb%d" % (t + 1)])
 
+    at(7.0)
     onehot(0)
+    at(3.6)
     for c in range(3):
         ts(ch(T.si, c % 2), ch(T.ptb, c), 4095, None, OP.bitwise_and, None, ["pt.%d" % c, "sf.%d" % (c - 2)], ["si.%d" % c], C)
         ts(ch(T.sf, c), ch(T.si, c % 2), -1024.0, None, OP.add, None, ["si.%d" % c], ["sf.%d" % c], C)
-    ts(T.t4[:, 256:384], T.t4[:, 256:384], 12, None, OP.bitwise_and, None, ["t4w"], ["t4w"], 128)
-    ts(T.t4[:, 0:256], T.t4[:, 0:256], 3, None, OP.bitwise_and, None, ["t4a"], ["t4a"], 256)
-    ts(T.e4[:], T.t4[:], 0.0, None, OP.is_equal, None, ["t4w", "t4a"], ["e4"], 384)
-    masked(T.ra, "ra", T.sf, "sf", 0, "id", 0)
-    compact(6, 0, T.zh, 0, T.ra, 0, ks("ra"))
     for c in range(3):
-        act(cx(m[1], c), cx(sw, c), AF.Abs, ["c0"], ["m1.%d" % c], n=WD[c])
-        dma("s", cx(T.mv, c), cx(m[1], c), ["m1.%d" % c], ["mv.%d" % c], WD[c] / 780)
-        act(cx(hh[1], c), cx(sw, c), AF.Sign, ["c0"], ["h1.%d" % c], bias=-EPS, scale=-1.0, n=WD[c])
-        act(cx(yy[1], c), cx(sw, c), AF.Identity, ["c0"], ["y1.%d" % c], bias=1.0, n=WD[c])
-    for j in range(4, 9):
-        dma("s", blk(T.aq, j, 1, V), T.s0[:], ks("mv"), ["aq%d" % j], 1.0)
-    act(m[1][:, V:W], sw[:, V:W], AF.Abs, ["c0.bus"], ["m1.bus"], n=W - V)
-    act(yy[1][:, V:W], sw[:, V:W], AF.Identity, ["c0.bus"], ["y1.bus"], bias=1.0, n=W - V)
-    onehot(1)
-    tt(blk(T.mb, 1, 1, 128), T.e4[:, 256:384], T.bd[:], OP.mult, ["e4", "bd"], ["w4"], 256)
-    tt(blk(T.mb, 2, 1, 128), T.e4[:, 0:128], T.bd[:], OP.mult, ["e4", "bd"], ["o4m"], 256)
+        at((7.5, 10.0, 10.4)[c])
+        ts(ch(T.ptb, c), ch(T.ptb, c), 2.0 ** -12, -1024.25, OP.mult, OP.add, ["pt.%d" % c, "si.%d" % c], ["ti.%d" % c], C)
+    at(8.0)
+    masked(T.ra, "ra", T.sf, "sf", ID, "id", 0)
+    k1024 = [(T.ih[:], T.kh[:])]
+    for h, (a, b) in enumerate(HALF):
+        at((8.2, 10.5)[h])
+        listed(1, h, [(T.ih[:], T.kh[:, a // 16:b // 16])] + sums(T.zh, 0, T.ra, 0, False, a, b),
+               ks("ra")[:1 + 2 * h] + ["z1", "ih", "k1024"])
+    at(6.4)
+    ts(T.t4[:, 256:384], T.t4[:, 256:384], 12, None, OP.bitwise_and, None, ["t4w"], ["t4w"], 128)
+    ts(T.t4[:, 0:256], T.t4[:, 0:256], 3, None, OP.bitwise_and, None, ["t4a", "t4b"], ["t4a"], 256)
+    ts(T.e4[:], T.t4[:], 0.0, None, OP.is_equal, None, ["t4w", "t4a"], ["e4"], 384)
+    tt(mat(W4), T.e4[:, 256:384], T.bd[:], OP.mult, ["e4", "bd"], ["w4"], 256)
+    at(18.0)
+    tt(mat(O4), T.e4[:, 0:128], T.bd[:], OP.mult, ["e4", "bd"], ["o4m"], 256)
     tt(T.mh[:], T.e4[:, 128:256], T.bd[:], OP.mult, ["e4", "bd"], ["fk"], 256)
     for c in range(3):
-        ts(ch(T.ptb, c), ch(T.ptb, c), 2.0 ** -12, -1024.25, OP.mult, OP.add, ["pt.%d" % c, "si.%d" % c], ["ti.%d" % c], C)
-    ts(blk(T.la, 0), blk(bank(6), 0), 1024.0, None, OP.add, None, ["#6"], ["la1"])
-    act(blk(T.qs, 0), blk(bank(6), 0), AF.Identity, ["#6"], ["qs0"], bias=1024.0)
+        at(5.0)
+        act(cx(hh[0], c), cx(sw, c), AF.Abs, ["sw"], ["h0.%d" % c], n=WD[c])
+        at((8.6, 10.9, 13.2)[c])
+        act(sign(1, c), cx(sw, c), AF.Sign, ["sw"], [signs(1)[c]], bias=-EPS, scale=-1.0, n=WD[c])
+        at((4.9, 12.4, 12.8)[c])
+        act(cx(yy[1], c), cx(sw, c), AF.Identity, ["sw"], ["y1.%d" % c], bias=0.5, scale=0.5, n=WD[c])
+        if c == 0:
+            send("y", [cx(yy[1], 0)], 1, ["y1.0"])
+    at(7.0)
+    dma("s", T.zp[:], hh[0][:, 0:V], ks("h0"), ks("zp"), 0.9)
+    at(9.0)
+    for j in range(2, 5):
+        dma("s", T.aq[:, SO + (j - 1) * V:SO + j * V], T.s0[:], ["oh0.0"], ["aq%d" % j], 0.9)
+    at(9.9)
+    act(hh[0][:, V:W], sw[:, V:W], AF.Abs, ["sw.bus"], ["h0.bus"], n=W - V)
+    at(17.0)
+    dma("s", T.aq[:, V:W], T.aq[:, AY + V:AY + W], ["ty"], ["tx", "sw.bus"], 0.45)
+    at(8.8)
+    onehot(1)
 
     product(1)
-    masked(rb[0], "rb0", T.sf, "sf", 1, "w4", 0)
     drive(1)
-    for c in range(3):
-        blend(1, c)
-    compact(7, 0, T.zb, 2, oh[0], 0, ks("oh0"))
-    compact(7, 1, T.zb, 2, oh[1], 0, ks("oh1"))
-    act(T.c0[:], blk(bank(7), 0, 2), AF.Identity, ["#7"], ["cur0"], n=2 * K)
-    act(T.c1[:], blk(bank(7), 0), AF.Identity, ["#7"], ["cur1"], bias=1.0)
-    for j in range(4):
-        compact(0, j, T.zh, 1 + j, rb[0], 0, ks("rb0"))
-    act(blk(T.qs, 1, 4), blk(bank(0), 0, 4), AF.Identity, ["#0"], ["qs1"], bias=1024.0, n=4 * K)
-    rows(1, 4)
-    masked(rb[1], "rb1", T.ptb, "ti", 1, "w4", 1)
-    for c in range(3):
-        bk = 1 + c % 2
-        pe([(bank(bk)[:], blk(T.mb, 2, 1, 128), ch(oh[1], c), True, True)], ["o4m", "oh1.%d" % c], ["#%d" % bk], C)
-        act(ch(T.aq, c), bank(bk)[:], AF.Identity, ["#%d" % bk], ["o4.%d" % c, "aq0"], n=C)
-    masked(T.ra, "ra", T.ptb, "ti", 0, "id", 1)
-    compact(6, 1, T.zh, 0, T.ra, 0, ks("ra"))
-    rows(0, 1)
-    ts(blk(T.vs, 0, 2), blk(T.vs, 0, 2), col[:, 0:1], None, OP.add, None, ["vs", "i"], ["vs0"])
-    ts(pv, blk(T.vs, 2), col[:, 9:10], None, OP.add, None, ["vs", "i96"], ["vv"])
-    cp(wid, blk(T.vs, 3), ["vs3"], ["vv"])
-    cp(blk(T.b5, 0, 2), blk(T.vs, 0, 2), ["vs0"], ["vv"])
-    cp(blk(T.ti, 0), blk(T.qs, 0), ["qs0"], ["ai"])
-    ts(blk(T.lb, 0), blk(bank(6), 1), 1024.0, None, OP.add, None, ["#6"], ["lb2"])
-    act(blk(T.qt, 0), blk(bank(6), 1), AF.Identity, ["#6"], ["qt0"], bias=1024.0)
-    fold()
+    at(11.7)
+    masked(T.rb0, "rb0", T.sf, "sf", W4, "w4", 0)
+    at(14.6)
+    masked(T.rt, "rt", T.ptb, "ti", ID, "id", 1)
+    at(16.5)
+    group(T.b7[:, 4:5 * K:5], sums(T.zh, 0, T.rt, 0), ks("rt") + ["z1"], 7)
+    at(18.5)
+    ts(blk(T.lb, 0), T.b7[:, 4:5 * K:5], 1024.0, None, OP.add, None, ["#7"], ["lb2"])
+    for j in range(5):
+        at((12.0, 13.5, 14.0, 15.0, 15.5)[j])
+        group(blk(T.b0, j), k1024 + (sums(T.zh, j, T.rb0, 0, True) if j else sums(T.zh, 0, T.ra, 0, True)),
+              ks("rb0" if j else "ra") + ["zh%d" % j if j else "z1", "ih", "k1024"], 0)
+    at(16.9)
+    act(T.qh[:], T.b0[:, 0:5 * K], AF.Identity, ["#0"], ["qh"], n=5 * K)
+    at(17.6)
+    tt(T.ql[:], T.b0[:, 0:5 * K], T.qh[:], OP.subtract, ["#0", "qh"], ["ql"], 5 * K)
+    at(16.0)
+    for j in range(2):
+        group(blk(T.b2, j), sums(T.zb, 2 + j, oh[0], SO), ks("oh0") + ["zb%d" % (2 + j)], 2)
+    at(19.0)
+    act(blk(T.kb, 8, 2), blk(T.b2, 0, 2), AF.Identity, ["#2"], ["r0"], n=2 * K)
+    at(17.7)
+    for j in range(5):
+        o = SO + (j - 1) * V if j else 0
+        was = [["sw"], ks("oh0")][j] if j < 2 else []
+        dma("s", T.aq[0:128:16, o:o + V], blk(T.qh, j), ["qh", "aq%d" % j], ["aqh%d" % j] + was, 0.25)
+        dma("s", T.aq[1:128:16, o:o + V], blk(T.ql, j), ["ql", "aq%d" % j], ["aql%d" % j] + was, 0.25)
+    at(19.2)
+    ts(blk(T.kb, 1), blk(T.kb, 0), 0.0, col[:, 0:1], OP.mult, OP.add, ["vhi", "i"], ["vlo"], 64)
+    ts(T.b6[:, 1:4 * K:4], blk(T.vs, 0), col[:, 0:1], -1.0, OP.add, OP.mult, ["vs0", "i", "#6"], ["nv"])
+    ts(T.b5[:, 1:2 * K:2], blk(T.vs, 1), col[:, 0:1], None, OP.add, None, ks("vs1") + ["i"], ["vl"])
+    ts(blk(T.b5, 2), blk(T.vs, 2), col[:, 0:1], None, OP.subtract, None, ks("vs2") + ["i"], ["wv"])
+    cp(T.b5[:, 0:2 * K:2], blk(T.vs, 3), ks("vs3"), ["bp"])
+    at(20.0)
     ahead(2)
-    ts(blk(T.tj, 0), blk(T.ti, 0), 15, None, OP.bitwise_and, None, ["ai"], ["alo"])
-    ts(blk(T.tj, 1), blk(T.ti, 0), 4, None, OP.arith_shift_right, None, ["ai"], ["ahi"])
-    ts(T.thr[:], blk(T.qs, 0), V - 0.5, 2.0, OP.is_ge, OP.mult, ["qs0"], ["thr"])
-    ts(l1, blk(T.tj, 0), float(K), None, OP.mult, None, ["alo"], ["l1"])
-    tt(T.pa[:], l1, blk(T.tj, 1), OP.add, ["l1", "ahi"], ["pa"])
-
-    for t in range(2, 6):
-        product(t)
-        trigger(t)
-        if t == 2:
-            tt(blk(T.dd, 0), T.pa[:], pv, OP.subtract, ["pa", "vv"], ["d1"])
-            tt(blk(T.dd, 1), T.nx2[:], T.pa[:], OP.subtract, ["pa", "nx2"], ["d3"], 2 * K)
-            tt(blk(T.dt, 0), blk(T.qt, 1), blk(T.qt, 0), OP.subtract, ["qt0", "qt1"], ["dt0"], 2 * K)
-        else:
-            prepare(t)
-        masks(t)
-        elect(t)
-        drive(t)
-        for c in range(3):
-            blend(t, c)
-        if t == 2:
-            tt(blk(T.b3, 0, 3), blk(T.qt, 2, 3), blk(T.qt, 1, 3), OP.subtract, ["qt1"], ["#3"], 6 * K)
-            tt(blk(T.f2, 0), blk(T.b3, 0), blk(T.dt, 0), OP.subtract, ["dt0", "#3"], ["f2"])
-            cp(blk(T.dt, 1, 2), blk(T.b3, 0, 2), ["#3"], ["dt1"], 2 * K)
-            tt(blk(T.f2, 1, 2), blk(T.b3, 1, 2), blk(T.dt, 1, 2), OP.subtract, ["dt1", "#3"], ["f2"], 2 * K)
-        cp(blk(T.la, t), blk(bank(6), 0), ["#6"], ["la%d" % (t + 1)])
-    product(6)
-    trigger(6)
-    prepare(6)
-    tt(T.ti[:], T.c0[:], T.jj[:], OP.add, ["cur0", "j"], ["ai", "ri"], 4 * K)
-    drive(6)
-    ts(T.tj[:], T.ti[:], 15, None, OP.bitwise_and, None, ["ai"], ["alo", "ahi"], 2 * K)
-    masks(6)
-    ts(T.tf[:], T.tj[:], 15.0, -16.0, OP.is_equal, OP.mult, ["alo"], ["tf"])
-    held(6)
-    ts(T.dd[:], T.tf[:], 1.0, None, OP.add, None, ["tf"], ["d1", "d3"])
-    tt(blk(T.bs, 1), T.be[:], vl, OP.add, ["be", "vv"], ["yl"])
-    tt(T.pr[:], blk(T.b7, 2, 2), T.dd[:], OP.mult, ["#7", "k36", "kh6", "d1"], ["pr"], 2 * K)
-    cp(blk(T.lb, 11), blk(T.bs, 1), ["yl"], ["lb7"])
-    tt(T.qq[:], T.pr[:], T.tj[:], OP.add, ["pr", "alo"], ["qq"], 4 * K)
-    blend(6, 0, "v")
-    ts(l1, blk(T.qq, 1), 16.0, None, OP.mult, None, ["qq"], ["l1"])
-    tt(T.qb[:], l1, blk(T.qq, 0), OP.add, ["qq", "l1"], ["qb"])
+    at(16.2)
+    masked(T.rb1, "rb1", T.ptb, "ti", W4, "w4", 1)
     for c in range(3):
-        pe([(bank(c)[0:8, i:C:16], T.mb[:, i:128:16], T.qb[:, 32 * c:32 * c + 32], True, True) for i in range(16)],
-           ["id", "qb"], ["#%d" % c], C)
-    blend(6, 1)
-    blend(6, 2, "v")
-    act(T.mv[0:8, 0:C], bank(0)[0:8, :], AF.Identity, ["#0"] + ks("sp0"), ["q0"], n=C)
-    act(T.mv[0:8, C:2 * C], bank(1)[0:8, :], AF.Identity, ["#1"] + ks("sp0"), ["q1"], n=C)
-    cp(T.mv[0:8, 2 * C:V], bank(2)[0:8, :], ["#2"] + ks("sp0"), ["q2"], C)
-    dma("s", T.q[:], T.mv[0:8, :], ["q0", "q1", "q2"], [])
+        bk = (2, 0, 2)[c]
+        at((19.3, 19.8, 24.5)[c])
+        pe([(bank(bk)[:], mat(O4), ch(oh[1], c), True, True)], ["o4m", "oh1.%d" % c], ["#%d" % bk])
+        act(ch(o4, c), bank(bk)[:], AF.Identity, ["#%d" % bk], ["o4.%d" % c, "fw0", "fw2"], n=C)
+    for c in range(3):
+        bk = 3 + c % 2
+        at((20.0, 20.5, 25.2)[c])
+        pe([(bank(bk)[:], T.mh[:], ch(T.rb1, c), True, True)], ["fk", "rb1.%d" % c], ["#%d" % bk])
+        tt(ch(T.ra, c), ch(o4, c), bank(bk)[:], OP.mult, ["#%d" % bk, "o4.%d" % c], ["ra.%d" % c], C)
+    at(START[2] + PLAN["turn"][1] - 2.0)
+    group(T.b7[:, 3:5 * K:5], sums(T.zh, 1, T.ra, 0) + sums(T.zh, 8, T.rt, 0), ks("ra") + ks("rt") + ["zh1", "zh8"], 7)
+
+    for t in range(2, 7):
+        trigger(t)
+        product(t)
+        if t < 6:
+            elect(t)
+        keep(t)
+        if t < 6:
+            turn(t)
+        drive(t)
+    steps = range(2, 7)
+    at(START[4] + 3.0)
+    group(blk(T.b4, 1), sums(T.zb, 3, oh[1], 0), ks("oh1") + ["zb3"], 4)
+    act(blk(T.ft, 1), blk(T.b4, 1), AF.Identity, ["#4", "fw1"], ["c0"])
+    at(START[6] + 3.0)
+    group(blk(T.b4, 0), [(mat(ID), blk(T.kb, 9))] + [(mat(NEG), slot(t, 3)) for t in steps],
+          ["r0", "id", "neg"] + ["n3%d" % t for t in steps], 4)
+    group(blk(T.b4, 1), [(mat(ID), blk(T.ft, 1))] + [(mat(ID), held(t)) for t in steps],
+          ["c0", "id"] + ["kh%d" % t for t in steps], 4)
+    ts(blk(T.wq, 0), blk(T.b4, 0), 15.5, -16.0, OP.is_ge, OP.mult, ["#4"], ["wp0"])
+    ts(blk(T.wq, 1), blk(T.b4, 1), 20.5, -16.0, OP.is_ge, OP.mult, ["#4"], ["wp1"])
+    tt(T.qb[:], T.b4[:, 0:2 * K], T.wq[:], OP.add, ["#4", "wp0", "wp1"], ["qb"], 2 * K)
+    group(T.b0[0:K, 0:128], [(blk(T.qb, 0), mat(ID)), (blk(T.qb, 1), mat(X16))], ["id", "x16", "qb"], 0)
+    act(T.gi[0:K, :], T.b0[0:K, 0:128], AF.Identity, ["#0", "lwm"], ["q"], bias=-80.0, n=128)
+
+    def store(s):
+        for j in range(8):
+            g.sync.dma_start(T.q[j, :], T.gi[0:K, 16 * j:16 * j + 16]).then_inc(s, 16)
+    add("s", store, ["q"], [], 0.5, DMA + 0.8, newsem(128), 0.4)
     issue()

import numpy as np
from concourse.bass import DstId, RemoteDMATransfer
from concourse.mybir import AluOpType as OP, ActivationFunctionType as AF

V, NB, W, C, K = 1536, 192, 2112, 512, 96
SH = {1: 1, 2: 3, 3: 6}
CH = [(0, 192), (192, 864), (864, 1536)]
WD = [b - a for a, b in CH]
HALF = [(0, NB), (NB, V)]
SO, AY = W, W + 4 * V
DK = 6 * K
EPS = 2.0 ** -26
EV = {t: (2,) for t in range(2, 6)}
CYC, PEC, GA, DMA, FAR, HOP, SELF = 0.00083, 0.6, 1.56, 2.0, 3.9, 0.12, 0.08
FIX = {"v": 0.03, "a": 0.06, "p": 0.1, "g": 0.15}
CASES = [(1.1, 1.15, 1.15, 1.15, 1.8), (1.45, 1.55, 1.0, 1.5, 1.0), (1.0, 1.45, 0.95, 1.0, 1.0)]
SEED, MOVES, HEAT, SOFT = 1, 70000, 0.05, 0.1
EARLY = dict.fromkeys("vapx", 30.0) | {"g": 1.5, "s": 2.5}
PERIOD = 8.6
START = {t: 10.0 + (t - 1) * PERIOD + (t > 1) * 1.2 for t in range(1, 7)}
PLAN = {"g1": (0.0, 2.1, 2.85), "g2": (1.85, 0.3, 1.05), "k": (3.7, 3.6), "e2": (0.4, 4.2, 5.5), "e3": (0.65, 2.9, 3.6),
        "e1": (0.9, 6.1, 5.2), "el": (4.6, 5.2, 6.7, 9.6), "keep": (4.3,), "turn": (4.1, 6.5), "g3": (4.0, 7.1, 5.8),
        "e4": (4.85, 10.3, 9.5), "add": (4.3,)}
FIRST = dict(PLAN, g1=(0.0, 1.6, 2.3), e2=(0.4, 2.5, 3.7), e3=(0.7, 3.1, 4.3), e1=(2.0, 5.8, 6.4), g3=(3.0, 6.4, 7.1),
             e4=(3.6, 8.8, 12.8), add=(5.0,))
LAST = dict(PLAN, g2=(1.0, -0.5, 0.25), g1=(2.8, 1.3, 2.0), k=(2.3, 2.2), keep=(2.4,), e1=(3.2, 2.1, 2.8), g3=(5.4, 3.9, 4.65),
            e4=(6.3, 4.7, 5.5))
ORDER, SCORE = [], []
F, B, H, I, U = "float32", "bfloat16", "float16", "int32", "uint16"


def sb(n, d):
    return ("sbuf", [128, n], d)


SCRATCH = {
    "ptb": sb(V, I), "si": sb(2 * C, I), "sf": sb(V, H), "oh1": sb(V, B),
    "ra": sb(V, H), "rb0": sb(V, H), "rb1": sb(V, H), "rt": sb(V, H), "fw": sb(2 * V, B),
    "pp": sb(V, F), "mv": sb(V, F), "zp": sb(V, B), "aq": sb(AY + W, B), "th": sb(W - V, B), "sg": sb(3 * NB, B),
    "sp0": sb(V, F), "sp1": sb(V, F),
    "t4": sb(384, I), "e4": sb(384, F), "one": sb(128, F), "bd1": sb(128, F), "bd": sb(128, F),
    "ci": sb(144, B), "gi": sb(128, F), "lw": sb(128, F), "pc": sb(6, I), "col": sb(16, F),
    "zb": sb(4 * 144, B), "zh": sb(9 * 144, H), "mb": sb(11 * 128, B), "mh": sb(128, H), "ih": sb(128, H),
    "curb": sb(K, I), "ci2": sb(2 * K, I), "ft": sb(4 * K, B), "vs": sb(4 * K, F),
    "kb": sb(10 * K, B), "kh": sb(K, H), "qh": sb(5 * K, B), "ql": sb(5 * K, B),
    "dk": sb(5 * DK, B), "dt": sb(5 * K, B), "so": sb(4 * K, F), "yo": sb(2 * K, F), "to": sb(5 * K, F),
    "wq": sb(2 * K, B), "qb": sb(2 * K, B),
    "la": sb(6 * K, U), "ll": sb(K, U), "lb": sb(5 * K, U), "ly": sb(5 * K, U),
    "df": ("dram", [11, 256, NB], F), "dh": ("dram", [7, 256, NB], B),
}
for _j in range(3):
    SCRATCH["m%d" % _j] = sb(W, F)
    SCRATCH["yy%d" % _j] = sb(W, F)
    SCRATCH["hh%d" % _j] = sb(W, B)
    SCRATCH["xv%d" % _j] = sb(6 * WD[_j], F)
for _j in range(8):
    SCRATCH["b%d" % _j] = ("psum", [128, C], F)

HANDS = [[("y", 1)] + [(k, t) for t in range(2, 7) for k in "my"], [("c", t) for t in range(2, 7)]]
SEMAPHORES = (["ev", "ea", "ep", "eg", "as1", "out"] + [x + k + str(t) for h in HANDS for k, t in h for x in "ha"]
              + ["d%d" % j for j in range(90)])


def mask_of(engines):
    return sum(1 << e for e in engines)


def apart(T, topo, rank):
    return [d for d in SH if T.cores[(rank + d) % len(T.cores)] not in topo.cores_of(T.cores[rank])]


def spread(g, core, T, topo, rank, stage, window, sem, local, back=None, ds=SH):
    n = len(T.cores)
    dst = {d: T.cores[(rank + d) % n] for d in [0] * (back is not None) + list(ds)}
    far = [d for d in dst if dst[d] not in topo.cores_of(core)]
    narrow = topo.engines(core, dst[far[0]]) if far else []
    trs, sent = [], 0
    for d in dst:
        kin = far if d in far else [x for x in dst if x not in far]
        pool = narrow if d in far else [e for e in topo.engines(core, dst[d]) if e not in narrow]
        q = kin.index(d)
        eng = pool[q * len(pool) // len(kin):(q + 1) * len(pool) // len(kin)]
        rid, pid = topo.addr(dst[d], core)
        row, o = (16 * SH[d], V + (d - 1) * NB) if d else (0, 0)
        trs.append(RemoteDMATransfer(dst_ids=[DstId(rid=rid, pnc=pid)], dma_engine_mask=mask_of(eng), remote_sem=sem,
                                     src=stage[row:row + 128, :], dst=(window if d else back)[:, o:o + NB]))
        sent += len(eng)
    g.remote_dma_fused(trs, local_sem=local)
    return sent


def arrange(ops):
    n = len(ops)
    qs = [o["q"] for o in ops]
    deps = [list(o["deps"].items()) for o in ops]
    kids = [[] for _ in ops]
    for i in range(n):
        for j, hard in deps[i]:
            kids[j].append((i, hard))

    def costs(cf, ga, dm, pc, lk):
        busy, lat = [], []
        for o in ops:
            f = cf * ga / GA if o["gather"] else pc if o["q"] == "p" else 1.0 if o["sem"] else cf
            busy.append(o["busy"] * f)
            lat.append(o["lat"] * (dm if o["sem"] else f) + o["port"] * (lk - 1))
        return busy, lat, [o["port"] * lk for o in ops]

    cases = [costs(*c) for c in CASES]
    move = [o["move"] for o in ops]
    firm = [[(j, HOP if qs[j] != qs[i] else SELF) for j, hard in deps[i] if hard] for i in range(n)]
    start, tight = [0.0] * n, []

    def ends(seq):
        out = 0.0
        for busy, lat, port in cases:
            free, done, pipe, link = dict.fromkeys("vapgsx", 0.0), [0.0] * n, 0.0, 0.0
            for i in seq:
                t = free[qs[i]]
                for j, gap in firm[i]:
                    if done[j] + gap > t:
                        t = done[j] + gap
                start[i] = t
                free[qs[i]] = t + busy[i]
                done[i] = t + lat[i]
                if move[i]:
                    pipe = max(pipe + move[i], done[i])
                    done[i] = pipe
                elif port[i]:
                    link = max(link + port[i], done[i])
                    done[i] = link
            out += max(done) + SOFT * sum(done) / n
        return out / len(cases)

    def longest(seq):
        pairs = []
        for busy, lat, port in cases:
            free, done, why, prev = dict.fromkeys("vapgsx", 0.0), [0.0] * n, [None] * n, {}
            for i in seq:
                t, why[i] = free[qs[i]], (prev.get(qs[i]), True)
                for j, gap in firm[i]:
                    if done[j] + gap > t:
                        t, why[i] = done[j] + gap, (j, False)
                free[qs[i]], done[i], prev[qs[i]] = t + busy[i], t + lat[i], i
            i = max(range(n), key=lambda k: done[k])
            while why[i][0] is not None:
                if why[i][1]:
                    pairs.append((why[i][0], i))
                i = why[i][0]
        return pairs

    def moved(seq):
        step = 1 if rng.randint(0, 2) else -1
        if tight and rng.randint(0, 3):
            a = seq.index(tight[int(rng.randint(0, len(tight)))][step < 0])
        else:
            a = int(rng.randint(0, n))
        i = seq[a]
        skip, b = int(rng.randint(1, 4)), a
        near = set(k for k, hard in (kids[i] if step > 0 else deps[i]))
        while skip:
            b += step
            if b < 0 or b >= n:
                return None
            skip -= qs[seq[b]] == qs[i]
        lo, hi = min(a, b), max(a, b)
        along, stay = [i], []
        for j in (seq[a + 1:hi + 1] if step > 0 else seq[lo:a][::-1]):
            if j in near:
                along.append(j)
                near.update(k for k, hard in (kids[j] if step > 0 else deps[j]))
            else:
                stay.append(j)
        if seq[b] in along:
            return None
        mid = stay + along if step > 0 else along[::-1] + stay[::-1]
        return seq[:lo] + mid + seq[hi + 1:]

    due = [o["due"] for o in ops]
    for i in range(n - 1, -1, -1):
        for j, hard in deps[i]:
            due[j] = min(due[j], due[i])

    def first(case, soon):
        busy, lat, port = case
        need, ready, free = [len(d) for d in deps], [0.0] * n, dict.fromkeys("vapgsx", 0.0)
        cand, seq, pipe, link = {q: [] for q in free}, [], 0.0, 0.0
        for i in range(n):
            if not need[i]:
                cand[qs[i]].append(i)
        while len(seq) < n:
            t0, q = min((max(free[q], min(max(ready[i], due[i] - EARLY[q]) for i in c)), q) for q, c in cand.items() if c)
            i = min((j for j in cand[q] if max(ready[j] - soon, due[j] - EARLY[q]) <= t0), key=lambda j: (due[j], j))
            cand[q].remove(i)
            seq.append(i)
            t = max(free[q], ready[i])
            free[q], done = t + busy[i], t + lat[i]
            if move[i]:
                pipe = done = max(pipe + move[i], done)
            elif port[i]:
                link = done = max(link + port[i], done)
            for k, hard in kids[i]:
                ready[k] = max(ready[k], done + (HOP if qs[k] != q else SELF) if hard else t)
                need[k] -= 1
                if not need[k]:
                    cand[qs[k]].append(k)
        return seq

    cur = best = min((first(c, s) for c in cases for s in (0.15, 0.3, 0.5, 0.8)), key=ends)
    now = score = ends(best)
    SCORE.append(score)
    rng = np.random.RandomState(SEED)
    for it in range(MOVES):
        if it % 100 == 0:
            ends(cur)
            cur = sorted(cur, key=lambda i: start[i])
            now = ends(cur)
        if it % 20 == 0:
            tight[:] = longest(cur)
        seq = moved(cur)
        if seq is None:
            continue
        s = ends(seq)
        if s <= now + HEAT * (1 - it / MOVES) * rng.exponential():
            cur, now = seq, s
            if s < score:
                best, score = seq, s
    SCORE.append(score)
    return best


def helpers(core, T, topo):
    return [c for c in topo.cores_of(core) if topo.die(c) == topo.die(core) and T.rank_of(c) is None][:3]


def feed(T, topo, rank, j):
    core = T.cores[rank]
    e = topo.engines(core, helpers(core, T, topo)[j])
    return e if j == 2 else e[j * len(e) // 2:(j + 1) * len(e) // 2]


def staged(T, k, t):
    return T.dh[t - 1] if k == "c" else T.df[t - 1 + 5 * (k == "m")]


def helper_program(g, core, T, topo, rank, j):
    sent = 0
    far = apart(T, topo, rank)
    for k, t in HANDS[j == 2]:
        g.wait_ge(T.sem["h%s%d" % (k, t)], 2 * len(feed(T, topo, rank, j)))
        win = T["hh%d" % ((t - 1) % 3)] if k == "c" else T["%s%d" % ("m" if k == "m" else "yy", t % 3)]
        sent += spread(g, core, T, topo, rank, staged(T, k, t), win, T.sem["a%s%d" % (k, t)], T.sem.out,
                       [None, T.mv if k == "m" else None, win][j], [[d for d in SH if d != far[1]], far[1:], SH][j])
    g.wait_ge(T.sem.out, sent)


def rank_program(g, core, T, topo):
    rank = T.rank_of(core)
    if rank is None:
        for r, c in enumerate(T.cores):
            hs = helpers(c, T, topo)
            if core in hs:
                helper_program(g, core, T, topo, r, hs.index(core))
        return
    hs = helpers(core, T, topo)
    nall = max(len(topo.engines(core, c)) for c in T.cores if c != core)
    Q = {"v": g.vector, "a": g.scalar, "p": g.tensor, "g": g, "s": g.sync}
    ops, last, readers, nd, due = [], {}, {}, [0], [0.0]

    def at(t, k=None, c=0):
        due[0] = t if k is None else START[t] + (FIRST if t == 1 else LAST if t == 6 else PLAN)[k][c]

    def add(q, fn, r, w, busy, lat, sem=None, move=0.0, port=0.0):
        deps = {}
        for k in list(w) + [k for k in r if k[0] == "#"]:
            for j in readers.get(k, []) + ([last[k]] if k in last else []):
                if k in w or ops[j]["q"] != q:
                    deps[j] = ops[j]["q"] != q or ops[j]["sem"] is not None
        for k in r:
            if k in last:
                deps[last[k]] = True
        for k in w:
            if k[0] == "~" and k in last:
                deps[last[k]] = False
        ops.append(dict(due=due[0], q=q, fn=fn, deps=deps, busy=busy, lat=lat, sem=sem, move=move, port=port,
                        gather=sem is None and any(k[:2] in ("la", "lb", "ll", "ly") for k in r)))
        for k in r:
            readers.setdefault(k, []).append(len(ops) - 1)
        for k in w:
            last[k] = len(ops) - 1
            readers[k] = []

    def op(q, fn, r, w, n=K):
        us = max(n, 64) * CYC + FIX[q]
        add(q, lambda s: fn().then_inc(s, 1), r, w, us, us)

    def newsem(n):
        nd[0] += 1
        return ("d%d" % (nd[0] - 1), n)

    def dma(q, out, in_, r, w, us=0.15, **kw):
        add(q, lambda s: Q[q].dma_start(out, in_, **kw).then_inc(s, 16), r, w, 1.0 if q == "g" else 0.06,
            DMA + us + (0.5 if q == "g" else 0.0), newsem(16), us)

    def send(k, srcs, t, r):
        trs, stage = [], staged(T, k, t)
        for j in ((2,) if k == "c" else (0, 1)):
            rid, pid = topo.addr(hs[j], core)
            trs.append(RemoteDMATransfer(dst_ids=[DstId(rid=rid, pnc=pid)] * 2, dma_engine_mask=mask_of(feed(T, topo, rank, j)),
                                         remote_sem=T.sem["h%s%d" % (k, t)], srcs=srcs, dsts=[stage[0:128, :], stage[128:256, :]],
                                         alu_op=1 if len(srcs) > 1 else 0))
        us = 0.7 if k == "c" else 1.3
        add("g", lambda s: g.remote_dma_fused(trs, local_sem=s), r, ["sent" + k + str(t)], 0.5, DMA + us, newsem(nall), us)

    def arrives(key, k, t):
        hand = HANDS[k == "c"]
        j = hand.index((k, t))
        add("x", None, ["sent%s%d" % x for x in hand[max(j - 1, 0):j + 1]], [key], 0.0, FAR + 2.0 * (j == 0),
            ("a%s%d" % (k, t), nall * {"c": 2, "m": 4, "y": 3}[k] // 2), 0.0, 0.9 if k == "c" else 1.8)

    def ts(out, in0, s1, s2, o0, o1, r, w, n=K):
        if o1 is None:
            op("v", lambda: g.vector.tensor_scalar(out, in0, s1, None, o0), r, w, n)
        else:
            op("v", lambda: g.vector.tensor_scalar(out, in0, s1, s2, o0, o1), r, w, n)

    def tt(out, a, b, o, r, w, n=K):
        op("v", lambda: g.vector.tensor_tensor(out, a, b, o), r, w, n)

    def cp(out, a, r, w, n=K):
        op("v", lambda: g.vector.tensor_copy(out, a), r, w, n)

    def scan(out, d0, d1, r, w, n):
        op("v", lambda: g.vector.tensor_tensor_scan(out, d0, d1, 0.0, OP.mult, OP.add), r, w, n)

    def act(out, a, f, r, w, bias=0.0, scale=1.0, n=K):
        op("a", lambda: g.scalar.activation(out, a, f, bias=bias, scale=scale), r, w, n)

    def pe(mms, r, w):
        def run():
            for a in mms:
                ins = g.tensor.matmul(*a)
            return ins
        op("p", run, r, w, PEC * sum(max(a[2].shape[1], min(64, a[1].shape[1])) for a in mms))

    def iota(out, pat, base, cm, w, flt=True):
        n = 2 * int(np.prod([p[1] for p in pat]))
        if flt:
            op("g", lambda: g.iota(out, pat, base, cm, allow_small_or_imprecise_dtypes=True), [], w, n)
        else:
            op("g", lambda: g.iota(out, pat, base, cm), [], w, n)

    def sel(out, a, pat, base, cm, r, w):
        op("g", lambda: g.affine_select(out, a, pat, OP.is_ge, 0.0, base, cm), r, w, 256)

    def issue():
        if not ORDER:
            ORDER.extend(arrange(ops))
        total, tok, waited = {}, {}, {q: {} for q in Q}
        for i in ORDER:
            o = ops[i]
            q = o["q"]
            s, c = o["sem"] or ("e" + q, total.get("e" + q, 0) + 1)
            total[s] = c
            tok[i] = (s, c)
            if q == "x":
                continue
            want = {}
            for j, hard in o["deps"].items():
                if hard:
                    want[tok[j][0]] = max(want.get(tok[j][0], 0), tok[j][1])
            for a, b in want.items():
                if waited[q].get(a, 0) < b:
                    Q[q].wait_ge(T.sem[a], b)
                    waited[q][a] = b
            o["fn"](T.sem[s])
        for s, c in total.items():
            g.wait_ge(T.sem[s], c)

    def blk(t, j, n=1, w=K):
        return t[:, j * w:(j + n) * w]

    def ch(t, c, o=0):
        return t[:, o + c * C:o + (c + 1) * C]

    def cx(t, c, o=0):
        return t[:, o + CH[c][0]:o + CH[c][1]]

    def lx(t, j, c):
        return t[:, j * K + CH[c][0] // 16:j * K + CH[c][1] // 16]

    def ks(n):
        return ["%s.%d" % (n, c) for c in range(3)]

    def bank(j):
        return T["b%d" % j]

    def mat(j):
        return blk(T.mb, j, 1, 128)

    def sums(z, zi, src, o, run=False, a=0, b=V):
        return [(z[:, zi * 144 + 15 - i:zi * 144 + 143 - i], src[:, o + i * K:o + (i + 1) * K] if run else src[:, o + a + i:o + b:16])
                for i in range(16)]

    def group(out, terms, r, bk):
        pe([(out, a, b, j == 0, j == len(terms) - 1) for j, (a, b) in enumerate(terms)], r, ["#%d" % bk])

    m = [T.m0, T.m1, T.m2]
    yy = [T.yy0, T.yy1, T.yy2]
    hh = [T.hh0, T.hh1, T.hh2]
    sp = [T.sp0, T.sp1]
    xv = [T.xv0, T.xv1, T.xv2]
    oh, oo = [T.aq, T.oh1], [SO, 0]
    col, sw = T.col, T.aq
    ID, W4, O4, NEG, LE, LW, P15, M15, X16, P60, M60 = range(11)
    o4 = T.fw

    def sign(j, c):
        return cx(hh[j], c) if c else blk(T.sg, j, 1, NB)

    def signs(j):
        return ["g%d" % j] + ks("h%d" % j)[1:]

    def slot(t, j):
        return T.dk[:, (t - 2) * DK + j:(t - 2) * DK + 4 * K:4]

    def held(t):
        return T.dk[:, (t - 2) * DK + 4 * K + 1:(t - 1) * DK:2]

    dma("s", T.curb[:], T.cur[:], [], ["cur", "~s"])
    dma("a", T.dh[0, 128:256, :], T.s0[:, 0:NB], [], ["dh1", "~a"])
    dma("s", T.dh[0, 0:128, :], T.s0[:, 0:NB], [], ["dh0", "~s"])
    dma("a", ch(T.ptb, 0), ch(T.pt, 0), [], ["pt.0", "~a"], 0.55)
    dma("s", sw[:, 0:V], T.s0[:], [], ["sw", "~s"], 0.9)
    dma("a", ch(T.ptb, 1), ch(T.pt, 1), [], ["pt.1", "~a"], 0.65)

    at(0.1)
    iota(T.pc[:, 0:1], [[0, 1]], 0, 1, ["pc"], False)
    iota(T.gi[:], [[1, 8], [0, 16]], 0, -1, ["gi"])
    iota(T.ci[:], [[1, 144]], 0, -1, ["ci"])
    iota(T.lw[:], [[0, 8], [-2, 16]], 0, 0, ["lw"])
    iota(T.pc[:, 1:2], [[0, 1]], 1, 1, ["pc1"], False)
    op("v", lambda: g.vector.memset(T.one[:], 1.0), [], ["one"])
    op("v", lambda: g.vector.memset(T.kh[:], 1024.0), [], ["k1024"], 64)
    ts(T.pc[:, 2:3], T.pc[:, 0:1], 15, None, OP.bitwise_and, None, ["pc"], ["pc2"], 64)
    ts(mat(LE), T.gi[:], 0.0, None, OP.is_equal, None, ["gi"], ["le"], 128)
    cp(col[:, 0:1], T.pc[:, 2:3], ["pc2"], ["i"], 64)
    ts(T.pc[:, 4:6], T.pc[:, 0:2], 3, None, OP.bitwise_and, None, ["pc", "pc1"], ["pc3"], 64)
    ts(col[:, 1:2], col[:, 0:1], -1.0, 15.0, OP.mult, OP.add, ["i"], ["c15"], 64)
    ts(col[:, 2:3], col[:, 0:1], col[:, 0:1], -1.0, OP.mult, OP.mult, ["i"], ["isq"], 64)
    ts(col[:, 3:4], col[:, 2:3], 1.0, None, OP.add, None, ["isq"], ["bias"], 64)
    ts(mat(ID), T.ci[:, 0:128], 0.0, None, OP.is_equal, None, ["ci"], ["id"], 64)
    ts(T.gi[:], T.gi[:], -8.0, None, OP.is_equal, None, ["gi", "le"], ["gi"], 128)
    tt(T.lw[:], T.gi[:], T.lw[:], OP.mult, ["gi", "lw"], ["lw"], 256)
    tt(mat(LW), mat(LE), T.lw[:], OP.add, ["le", "lw"], ["lwm"], 256)
    ts(blk(T.zh, 0, 1, 144), T.ci[:], col[:, 1:2], None, OP.is_equal, None, ["ci", "c15"], ["z1"], 72)
    ts(T.ih[:], T.ci[:, 0:128], 0.0, None, OP.is_equal, None, ["ci"], ["ih"], 64)
    at(1.5)
    act(T.kb[:, 7 * K:7 * K + 1], col[:, 0:1], AF.Sigmoid, ["i"], ["wa"], bias=384.0, scale=-256.0, n=1600)
    for j in range(4):
        ts(col[:, 5 + j:6 + j], T.pc[:, 4:5], float(j), None, OP.is_equal, None, ["pc3"], ["wq%d" % j], 64)
    cp(col[:, 9:10], T.pc[:, 5:6], ["pc3"], ["wr"], 64)
    act(col[:, 10:11], col[:, 0:1], AF.Identity, ["i"], ["w5"], bias=5.0, n=64)
    for j, x, k in ((NEG, -1.0, "neg"), (P15, float(V), "p15"), (M15, -float(V), "m15"), (X16, 16.0, "x16"),
                    (P60, 4.0 * V, "p60"), (M60, -4.0 * V, "m60")):
        act(mat(j), mat(ID), AF.Identity, ["id"], [k], scale=x, n=128)
    sel(T.bd1[:], T.one[:], [[16, 8], [0, 16]], 15, -1, ["one"], ["bd1"])
    iota(T.t4[:, 256:384], [[1, 128]], 255, -1, ["t4w"], False)
    at(2.4)
    add("g", lambda s: spread(g, core, T, topo, rank, T.dh[0], sw, T.sem.as1, s), ["dh0", "dh1"], ["sent0.0"], 2.0, FAR + 1.5, newsem(nall))
    add("x", None, ["sent0.0"], ["sw.bus"], 0.0, 0.3, ("as1", nall))

    for tb, (o, x) in enumerate(((OP.bitwise_and, 15), (OP.arith_shift_right, 4))):
        at(1.0 + 0.1 * tb)
        ts(blk(T.ci2, tb), T.curb[:], x, None, o, None, ["cur"], ["ci%d" % tb])
        cp(blk(T.ft, 2 + tb), blk(T.ci2, tb), ["ci%d" % tb], ["f%d" % (2 + tb)])
        act(blk(T.ft, tb), blk(T.ft, 2 + tb), AF.Square, ["f%d" % (2 + tb)], ["f%d" % tb])
        for f, q in ((2 + tb, "s"), (tb, "a")):
            dma(q, T.fw[f // 2 * 8:f // 2 * 8 + 8, tb * V:(tb + 1) * V], blk(T.ft, f), ["f%d" % f], ["fw%d" % f], 0.25)
        if tb == 0:
            dma("s", ch(T.ptb, 2), ch(T.pt, 2), ["f0"], ["pt.2"], 0.65)

    z0, zhalf = blk(T.zh, 0, 1, 144), blk(T.zb, 0, 1, 144)
    at(8.5)
    tt(col[:, 11:14], col[:, 6:9], col[:, 5:8], OP.subtract, ["wq%d" % j for j in range(4)], ["wd"], 64)
    for j in range(7):
        c = 5 + j if j < 4 else 7 + j
        ts(blk(T.zh, 1 + j, 1, 144), z0, col[:, c:c + 1], None, OP.mult, None, ["z1", "wq%d" % j if j < 4 else "wd"], ["zh%d" % (1 + j)], 72)
    ts(blk(T.zh, 8, 1, 144), z0, -1.0, None, OP.mult, None, ["z1"], ["zh8"], 72)
    ts(zhalf, z0, 0.5, None, OP.mult, None, ["z1"], ["zb0"], 72)
    ts(col[:, 14:16], col[:, 9:11], 2.0, None, OP.mult, None, ["wr", "w5"], ["w2"], 64)
    ts(blk(T.zb, 1, 1, 144), z0, T.kb[:, 7 * K:7 * K + 1], None, OP.mult, None, ["z1", "wa"], ["zb1"], 72)
    at(14.0)
    act(blk(T.zb, 2, 1, 144), zhalf, AF.Identity, ["zb0", "w2"], ["zb2"], scale=col[:, 14:15], n=144)
    act(blk(T.zb, 3, 1, 144), zhalf, AF.Identity, ["zb0", "w2"], ["zb3"], scale=col[:, 15:16], n=144)
    at(4.5)
    sel(T.bd[:], T.bd1[:], [[-16, 8], [0, 16]], 0, 1, ["bd1"], ["bd"])
    iota(T.t4[:, 0:128], [[0, 8], [1, 4], [0, 4]], 255, -1, ["t4a"], False)
    iota(T.t4[:, 128:256], [[0, 8], [1, 4], [1, 4]], 256, -1, ["t4b"], False)
    at(8.0)
    iota(blk(T.vs, 0), [[16, K]], 0, 0, ["vs0"])
    at(15.5)
    for c in range(3):
        n = WD[c] // 16
        iota(lx(T.vs, 1, c), [[16, n]], 0, 0, ["vs1.%d" % c])
        iota(lx(T.vs, 2, c), [[-16, n]], WD[c], 0, ["vs2.%d" % c])
        iota(lx(T.vs, 3, c), [[0, n]], WD[c], 0, ["vs3.%d" % c])
    at(8.5)
    iota(blk(T.kb, 0), [[16, K]], 0, 0, ["vhi"])
    iota(T.th[:], [[64, 9], [0, 64]], V, 0, ["th"])
    iota(T.aq[:, AY + V:AY + W], [[0, 9], [1, 64]], 0, 0, ["ty"])
    at(11.0)
    dma("s", T.aq[0:128:16, AY + V:AY + W], T.th[0:128:16, :], ["th", "ty"], ["ty"], 0.25)
    for t in range(2, 7):
        at(7.5 if t == 2 else START[t - 1] + 7.5)
        if t < 6:
            iota(T.dk[:, (t - 2) * DK:(t - 2) * DK + 4 * K], [[0, K], [1, 4]], 0, 0, ["k1%d" % t, "n3%d" % t])
        iota(T.dk[:, (t - 2) * DK + 4 * K:(t - 1) * DK], [[0, K], [1, 2]], 0, 0, ["kh%d" % t])
    for t in range(2, 6):
        at(START[t - 1] + 3.5)
        iota(blk(T.kb, t + 1), [[0, K]], (t - 2) * V + (SO if t % 2 == 0 else SO - AY), 0, ["ck%d" % t])
    at(20.0)
    iota(T.dt[:], [[0, 5 * K]], 0, 0, ["dt"])

    def onehot(tb):
        for c in range(3):
            pe([(bank(c)[:], T.mb[0:16, LW * 128:(LW + 1) * 128], T.fw[0:16, tb * V + c * C:tb * V + (c + 1) * C], True, True)],
               ["lwm", "fw%d" % tb, "fw%d" % (2 + tb)], ["#%d" % c])
            act(ch(oh[tb], c, oo[tb]), bank(c)[:], AF.Relu, ["#%d" % c, "bias"], ["oh%d.%d" % (tb, c)], bias=col[:, 3:4], scale=-1.0, n=C)

    def masked(out, on, tab, tn, mt, mn, tb):
        for c in range(3):
            bk = 3 + c % 2
            pe([(bank(bk)[:], mat(mt), ch(oh[tb], c, oo[tb]), True, True)], [mn, "oh%d.%d" % (tb, c)], ["#%d" % bk])
            tt(ch(out, c), ch(tab, c), bank(bk)[:], OP.mult, ["#%d" % bk, "%s.%d" % (tn, c)], ["%s.%d" % (on, c)], C)

    def la(t, c):
        j = 0 if t < 3 else t - 1
        return lx(T.la, j, c), "la%d.%d" % (j + 1, c > 0)

    def listed(t, h, terms, r):
        a, b = HALF[h][0] // 16, HALF[h][1] // 16
        group(T.b6[:, 4 * a:4 * b:4], terms, r, 6)
        cp(T.la[:, (t - 1) * K + a:(t - 1) * K + b], T.b6[:, 4 * a:4 * b:4], ["#6"], ["la%d.%d" % (t, h)], b - a)

    def product(t):
        mt, n, u = m[t % 3], "m%d" % (t % 3), (t + 1) % 3
        e = 1.0 if t % 2 else -1.0
        mv, vn = T.mv, ks("mv")
        at(t, "g1")
        if t > 1:
            arrives(n + ".bus", "m", t)
            vn[0] = n + ".bus"
        else:
            mt, n, mv, vn = hh[0], "h0", T.zp, ks("zp")
        for c in range(3):
            o, on = la(t, c)
            at(t, "g1", c)
            tt(cx(T.pp, c), mt[:, 0:W].indirect(o), cx(mv, c), OP.mult, ks(n) + [n + ".bus", on, vn[c]], ["p.%d" % c], GA * WD[c])
        for c in range(3):
            if t < 6:
                at(t, "e2", c)
                act(cx(m[u], c), cx(T.pp, c), AF.Abs, ["p.%d" % c], ["m%d.%d" % (u, c)], bias=1.0, scale=-2.0, n=WD[c])
                if c == 0:
                    send("m", [cx(m[u], 0)], t + 1, ["m%d.0" % u])
                else:
                    dma("s", cx(T.mv, c), cx(m[u], c), ["m%d.%d" % (u, c)], ["mv.%d" % c], 0.75)
                at(t, "e3", c)
                act(sign(u, c), cx(T.pp, c), AF.Sign, ["p.%d" % c], [signs(u)[c]], bias=e * (1.875 + 2.0 ** -23), scale=-3.75 * e, n=WD[c])
                if c == 0:
                    send("c", [sign(t % 3, 0), sign(u, 0)], t + 1, ["g%d" % (t % 3), "g%d" % u])
            at(t, "e1", c)
            if c in EV.get(t, ()):
                ts(cx(sp[t % 2], c), cx(T.pp, c), -2.0, 1.0, OP.mult, OP.add, ["p.%d" % c], ["sp%d.%d" % (t % 2, c)], WD[c])
            else:
                act(cx(sp[t % 2], c), cx(T.pp, c), AF.Identity, ["p.%d" % c], ["sp%d.%d" % (t % 2, c)], bias=1.0, scale=-2.0, n=WD[c])
        if t < 6:
            at(t, "add")
            dma("g", hh[t % 3][:, NB:V], hh[u][:, NB:V], ks("h%d" % u)[1:] + ks("h%d" % (t % 3))[1:], ks("h%d" % (t % 3))[1:], 1.2,
                accum_op=OP.add)

    def drive(t):
        yt, n, u = yy[t % 3], "y%d" % (t % 3), (t + 1) % 3
        at(t, "g3")
        arrives(n + ".bus", "y", t)
        for c in range(3):
            o, on = la(t, c)
            w = WD[c]
            at(t, "g3", c)
            tt(blk(xv[c], 6 - t, 1, w), yt[:, 0:W].indirect(o), cx(sp[t % 2], c), OP.mult,
               ks(n) + [n + ".bus", on, "sp%d.%d" % (t % 2, c)], ["x%d.%d" % (t, c)], GA * w)
            at(t, "e4", c)
            vs = ["x%d.%d" % (j, c) for j in range(1, t + 1)] + ["ly%d" % t] * (t > 1)
            src = blk(xv[c], 5, 1, w) if t == 1 else xv[c][:, (6 - t) * w:6 * w].indirect(lx(T.ly, t - 2, c))
            if t < 6:
                act(cx(yy[u], c), src, AF.Sigmoid, vs, ["y%d.%d" % (u, c)], scale=4.0, n=w * GA if t > 1 else w)
                if c == 0:
                    send("y", [cx(yy[u], 0)], t + 1, ["y%d.0" % u])
            else:
                act(cx(m[1], c), src, AF.Sigmoid, vs, ["m1.%d" % c], scale=4.0, n=w * GA)
                ts(cx(m[1], c), cx(m[1], c), 2.0, -1.0, OP.mult, OP.add, ["m1.%d" % c], ["m1.%d" % c], w)
                dma("s", cx(T.y, c), cx(m[1], c), ["m1.%d" % c], [], w / 1100)

    def trigger(t):
        w, n = hh[(t - 1) % 3], "h%d" % ((t - 1) % 3)
        at(t, "g2")
        arrives(n + ".bus", "c", t)
        for c in range(3):
            at(t, "g2", c)
            tt(cx(T.zp, c), w[:, 0:W].indirect(lx(T.lb, t - 2, c)), sign(t % 3, c), OP.mult,
               ks(n) + [n + ".bus", "lb%d" % t, signs(t % 3)[c]], ["zp.%d" % c], GA * WD[c])
        z = blk(T.b1, 0)
        group(z, sums(T.zb, 0, T.zp, 0), ks("zp") + ["zb0"], 1)
        at(t, "k")
        if t < 6:
            ts(slot(t, 2), z, 0.5, None, OP.is_ge, None, ["#1"], ["k1%d" % t])
        ts(slot(t, 3), z, 2.5, None, OP.is_le, None, ["#1"], ["n3%d" % t])
        at(t, "k", 1)
        ts(held(t), z, -1.5, None, OP.is_le, None, ["#1"], ["kh%d" % t])

    def ahead(t):
        turns = [slot(j, 3) for j in range(2, t)]
        r = ["id", "neg", "p15", "m15", "r0", "ck%d" % t, "vhi", "vlo"] + ["n3%d" % j for j in range(2, t)]
        r0, wrap = blk(T.kb, 8), [blk(T.kb, 2)] * (t > 2)
        if t > 2:
            group(blk(T.b2, 2), [(mat(ID), r0)] + [(mat(NEG), x) for x in turns], r, 2)
            act(wrap[0], blk(T.b2, 2), AF.Sigmoid, ["#2"], ["wrap"], bias=256.0 * (t - 5.5), scale=256.0)
            r = r + ["wrap", "p60", "m60"]
        group(T.b6[:, 2:4 * K:4], [(mat(NEG), blk(T.kb, t + 1)), (mat(M15), r0)] + [(mat(P15), x) for x in turns]
              + [(mat(P60), x) for x in wrap], r, 6)
        group(T.b6[:, 3:4 * K:4], [(mat(ID), blk(T.kb, j)) for j in (t + 1, 0, 1)] + [(mat(P15), r0)]
              + [(mat(M15), x) for x in turns] + [(mat(M60), x) for x in wrap], r, 6)

    def elect(t):
        even = t % 2 == 0
        at(t, "el")
        scan(T.so[:], T.dk[:, (t - 2) * DK:(t - 2) * DK + 4 * K], T.b6[:, 0:4 * K], ["#6", "k1%d" % t, "n3%d" % t, "nv"], ["so"], 4 * K)
        ts(T.ll[:], T.so[:, 3:4 * K:4], 0.0 if even else float(AY - SO), None, OP.add, None, ["so"], ["ll"])
        win = T.aq[:, 0:AY] if even else T.aq[:, SO:AY + W]
        o = AY if even else 0
        tabs = ["aq%s%d" % (x, j) for x in "hl" for j in range(1, 5)]
        old, new = ("ax", "ay") if even else ("ay", "ax")
        for h, (a, b) in enumerate(HALF):
            at(t, "el", 1 + h)
            act(T.aq[:, o + a:o + b], win.indirect(T.ll[:, a // 16:b // 16]), AF.Identity,
                ["ll", old + "0", old + "1"] + tabs + (["tx", "aqh0", "aql0"] if even else ["ty"]), [new + str(h)], n=GA * (b - a))
            listed(t + 1, h, sums(T.zb, 1, T.aq, o, False, a, b), [new + str(h), "zb1"])
        if t < 5:
            at(t, "el", 3)
            ahead(t + 1)

    def keep(t):
        at(t, "keep")
        scan(T.yo[:], T.dk[:, (t - 2) * DK + 4 * K:(t - 1) * DK], T.b5[:, 0:2 * K], ["kh%d" % t, "bp", "vl"], ["yo"], 2 * K)
        cp(blk(T.ly, t - 2), T.yo[:, 1:2 * K:2], ["yo"], ["ly%d" % t])
        if t < 6:
            tt(T.b5[:, 0:2 * K:2], T.yo[:, 1:2 * K:2], blk(T.b5, 2), OP.add, ["yo", "wv"], ["bp"])

    def turn(t):
        at(t, "turn")
        if t == 2:
            at(t, "turn", 1)
            tt(blk(T.to, 0), T.b7[:, 3:5 * K:5], held(t), OP.mult, ["#7", "kh2"], ["to0"])
            tt(blk(T.to, 1), T.b7[:, 4:5 * K:5], blk(T.to, 0), OP.add, ["#7", "to0"], ["to"])
            ts(blk(T.lb, 1), blk(T.to, 1), 1024.0, None, OP.add, None, ["to"], ["lb3"])
            at(START[3] + 1.0)
            for k in range(1, 4):
                group(T.b7[:, 3 - k:5 * K:5], sums(T.zh, 4 + k, T.ra, 0), ks("ra") + ["zh%d" % (4 + k)], 7)
            return
        group(blk(T.b3, 0), [(mat(ID), held(j)) for j in range(2, t + 1)], ["id"] + ["kh%d" % j for j in range(2, t + 1)], 3)
        for k in range(1, t):
            act(T.dt[:, 5 - k:5 * K:5], blk(T.b3, 0), AF.Sigmoid, ["#3", "dt"], ["dt%d" % k], bias=128.0 - 256.0 * k, scale=256.0)
        at(t, "turn", 1)
        scan(T.to[:], T.dt[:], T.b7[:, 0:5 * K], ["#7", "dt"] + ["dt%d" % k for k in range(1, t)], ["to"], 5 * K)
        ts(blk(T.lb, t - 1), T.to[:, 4:5 * K:5], 1024.0, None, OP.add, None, ["to"], ["lb%d" % (t + 1)])

    at(7.0)
    onehot(0)
    at(3.6)
    for c in range(3):
        ts(ch(T.si, c % 2), ch(T.ptb, c), 4095, None, OP.bitwise_and, None, ["pt.%d" % c, "sf.%d" % (c - 2)], ["si.%d" % c], C)
        ts(ch(T.sf, c), ch(T.si, c % 2), -1024.0, None, OP.add, None, ["si.%d" % c], ["sf.%d" % c], C)
    for c in range(3):
        at((7.5, 10.0, 10.4)[c])
        ts(ch(T.ptb, c), ch(T.ptb, c), 2.0 ** -12, -1024.25, OP.mult, OP.add, ["pt.%d" % c, "si.%d" % c], ["ti.%d" % c], C)
    at(8.0)
    masked(T.ra, "ra", T.sf, "sf", ID, "id", 0)
    k1024 = [(T.ih[:], T.kh[:])]
    for h, (a, b) in enumerate(HALF):
        at((8.2, 10.5)[h])
        listed(1, h, [(T.ih[:], T.kh[:, a // 16:b // 16])] + sums(T.zh, 0, T.ra, 0, False, a, b),
               ks("ra")[:1 + 2 * h] + ["z1", "ih", "k1024"])
    at(6.4)
    ts(T.t4[:, 256:384], T.t4[:, 256:384], 12, None, OP.bitwise_and, None, ["t4w"], ["t4w"], 128)
    ts(T.t4[:, 0:256], T.t4[:, 0:256], 3, None, OP.bitwise_and, None, ["t4a", "t4b"], ["t4a"], 256)
    ts(T.e4[:], T.t4[:], 0.0, None, OP.is_equal, None, ["t4w", "t4a"], ["e4"], 384)
    tt(mat(W4), T.e4[:, 256:384], T.bd[:], OP.mult, ["e4", "bd"], ["w4"], 256)
    at(18.0)
    tt(mat(O4), T.e4[:, 0:128], T.bd[:], OP.mult, ["e4", "bd"], ["o4m"], 256)
    tt(T.mh[:], T.e4[:, 128:256], T.bd[:], OP.mult, ["e4", "bd"], ["fk"], 256)
    for c in range(3):
        at(5.0)
        act(cx(hh[0], c), cx(sw, c), AF.Abs, ["sw"], ["h0.%d" % c], n=WD[c])
        at((8.6, 10.9, 13.2)[c])
        act(sign(1, c), cx(sw, c), AF.Sign, ["sw"], [signs(1)[c]], bias=-EPS, scale=-1.0, n=WD[c])
        at((4.9, 12.4, 12.8)[c])
        act(cx(yy[1], c), cx(sw, c), AF.Identity, ["sw"], ["y1.%d" % c], bias=0.5, scale=0.5, n=WD[c])
        if c == 0:
            send("y", [cx(yy[1], 0)], 1, ["y1.0"])
    at(7.0)
    dma("s", T.zp[:], hh[0][:, 0:V], ks("h0"), ks("zp"), 0.9)
    at(9.0)
    for j in range(2, 5):
        dma("s", T.aq[:, SO + (j - 1) * V:SO + j * V], T.s0[:], ["oh0.0"], ["aq%d" % j], 0.9)
    at(9.9)
    act(hh[0][:, V:W], sw[:, V:W], AF.Abs, ["sw.bus"], ["h0.bus"], n=W - V)
    at(17.0)
    dma("s", T.aq[:, V:W], T.aq[:, AY + V:AY + W], ["ty"], ["tx", "sw.bus"], 0.45)
    at(8.8)
    onehot(1)

    product(1)
    drive(1)
    at(11.7)
    masked(T.rb0, "rb0", T.sf, "sf", W4, "w4", 0)
    at(14.6)
    masked(T.rt, "rt", T.ptb, "ti", ID, "id", 1)
    at(16.5)
    group(T.b7[:, 4:5 * K:5], sums(T.zh, 0, T.rt, 0), ks("rt") + ["z1"], 7)
    at(18.5)
    ts(blk(T.lb, 0), T.b7[:, 4:5 * K:5], 1024.0, None, OP.add, None, ["#7"], ["lb2"])
    for j in range(5):
        at((12.0, 13.5, 14.0, 15.0, 15.5)[j])
        group(blk(T.b0, j), k1024 + (sums(T.zh, j, T.rb0, 0, True) if j else sums(T.zh, 0, T.ra, 0, True)),
              ks("rb0" if j else "ra") + ["zh%d" % j if j else "z1", "ih", "k1024"], 0)
    at(16.9)
    act(T.qh[:], T.b0[:, 0:5 * K], AF.Identity, ["#0"], ["qh"], n=5 * K)
    at(17.6)
    tt(T.ql[:], T.b0[:, 0:5 * K], T.qh[:], OP.subtract, ["#0", "qh"], ["ql"], 5 * K)
    at(16.0)
    for j in range(2):
        group(blk(T.b2, j), sums(T.zb, 2 + j, oh[0], SO), ks("oh0") + ["zb%d" % (2 + j)], 2)
    at(19.0)
    act(blk(T.kb, 8, 2), blk(T.b2, 0, 2), AF.Identity, ["#2"], ["r0"], n=2 * K)
    at(17.7)
    for j in range(5):
        o = SO + (j - 1) * V if j else 0
        was = [["sw"], ks("oh0")][j] if j < 2 else []
        dma("s", T.aq[0:128:16, o:o + V], blk(T.qh, j), ["qh", "aq%d" % j], ["aqh%d" % j] + was, 0.25)
        dma("s", T.aq[1:128:16, o:o + V], blk(T.ql, j), ["ql", "aq%d" % j], ["aql%d" % j] + was, 0.25)
    at(19.2)
    ts(blk(T.kb, 1), blk(T.kb, 0), 0.0, col[:, 0:1], OP.mult, OP.add, ["vhi", "i"], ["vlo"], 64)
    ts(T.b6[:, 1:4 * K:4], blk(T.vs, 0), col[:, 0:1], -1.0, OP.add, OP.mult, ["vs0", "i", "#6"], ["nv"])
    ts(T.b5[:, 1:2 * K:2], blk(T.vs, 1), col[:, 0:1], None, OP.add, None, ks("vs1") + ["i"], ["vl"])
    ts(blk(T.b5, 2), blk(T.vs, 2), col[:, 0:1], None, OP.subtract, None, ks("vs2") + ["i"], ["wv"])
    cp(T.b5[:, 0:2 * K:2], blk(T.vs, 3), ks("vs3"), ["bp"])
    at(20.0)
    ahead(2)
    at(16.2)
    masked(T.rb1, "rb1", T.ptb, "ti", W4, "w4", 1)
    for c in range(3):
        bk = (2, 0, 2)[c]
        at((19.3, 19.8, 24.5)[c])
        pe([(bank(bk)[:], mat(O4), ch(oh[1], c), True, True)], ["o4m", "oh1.%d" % c], ["#%d" % bk])
        act(ch(o4, c), bank(bk)[:], AF.Identity, ["#%d" % bk], ["o4.%d" % c, "fw0", "fw2"], n=C)
    for c in range(3):
        bk = 3 + c % 2
        at((20.0, 20.5, 25.2)[c])
        pe([(bank(bk)[:], T.mh[:], ch(T.rb1, c), True, True)], ["fk", "rb1.%d" % c], ["#%d" % bk])
        tt(ch(T.ra, c), ch(o4, c), bank(bk)[:], OP.mult, ["#%d" % bk, "o4.%d" % c], ["ra.%d" % c], C)
    at(START[2] + PLAN["turn"][1] - 2.0)
    group(T.b7[:, 3:5 * K:5], sums(T.zh, 1, T.ra, 0) + sums(T.zh, 8, T.rt, 0), ks("ra") + ks("rt") + ["zh1", "zh8"], 7)

    for t in range(2, 7):
        trigger(t)
        product(t)
        if t < 6:
            elect(t)
        keep(t)
        if t < 6:
            turn(t)
        drive(t)
    steps = range(2, 7)
    at(START[4] + 3.0)
    group(blk(T.b4, 1), sums(T.zb, 3, oh[1], 0), ks("oh1") + ["zb3"], 4)
    act(blk(T.ft, 1), blk(T.b4, 1), AF.Identity, ["#4", "fw1"], ["c0"])
    at(START[6] + 3.0)
    group(blk(T.b4, 0), [(mat(ID), blk(T.kb, 9))] + [(mat(NEG), slot(t, 3)) for t in steps],
          ["r0", "id", "neg"] + ["n3%d" % t for t in steps], 4)
    group(blk(T.b4, 1), [(mat(ID), blk(T.ft, 1))] + [(mat(ID), held(t)) for t in steps],
          ["c0", "id"] + ["kh%d" % t for t in steps], 4)
    ts(blk(T.wq, 0), blk(T.b4, 0), 15.5, -16.0, OP.is_ge, OP.mult, ["#4"], ["wp0"])
    ts(blk(T.wq, 1), blk(T.b4, 1), 20.5, -16.0, OP.is_ge, OP.mult, ["#4"], ["wp1"])
    tt(T.qb[:], T.b4[:, 0:2 * K], T.wq[:], OP.add, ["#4", "wp0", "wp1"], ["qb"], 2 * K)
    group(T.b0[0:K, 0:128], [(blk(T.qb, 0), mat(ID)), (blk(T.qb, 1), mat(X16))], ["id", "x16", "qb"], 0)
    act(T.gi[0:K, :], T.b0[0:K, 0:128], AF.Identity, ["#0", "lwm"], ["q"], bias=-80.0, n=128)

    def store(s):
        for j in range(8):
            g.sync.dma_start(T.q[j, :], T.gi[0:K, 16 * j:16 * j + 16]).then_inc(s, 16)
    add("s", store, ["q"], [], 0.5, DMA + 0.8, newsem(128), 0.4)
    issue()
